import numpy as np
import ml_dtypes


def mxq(x, axis, fmt="e4m3"):
    dtype, down = {"e4m3": (ml_dtypes.float8_e4m3fn, 7), "e5m2": (ml_dtypes.float8_e5m2, 14)}[fmt]
    v = np.moveaxis(np.asarray(x, np.float32).astype(ml_dtypes.bfloat16).astype(np.float64), axis, -1)
    blocks = v.reshape(v.shape[:-1] + (-1, 32))
    amax = np.abs(blocks).max(-1, keepdims=True)
    byte = np.maximum(np.where(amax > 0, np.frexp(amax)[1] - 1 + 127, 0) - down, 1)
    scale = np.exp2(byte - 127.0)
    codes = (blocks / scale).astype(np.float32).astype(dtype).astype(np.float64)
    return np.moveaxis((codes * scale).reshape(v.shape), -1, axis)


WIDE = False


def mx_kscale(k):
    if not WIDE:
        return np.ones(k)
    levels = np.array([10, -10, 5, -5, 0])
    if k % 512:
        return np.exp2(np.random.permutation(np.resize(levels, k // 32))).repeat(32)
    a = np.empty((k // 512, 16))
    for p in range(k // 512):
        a[p, :8] = np.random.permutation(np.resize(levels, 8))
        for g in range(8):
            far = levels[np.abs(levels - a[p, g]) >= 10]
            a[p, g + 8] = far[np.random.randint(len(far))]
    return np.exp2(a.ravel()).repeat(32)


def f64(x):
    return np.asarray(x).astype(np.float64)


def striped(idx):
    return np.tile(idx.reshape(-1, 16).T, (8, 1)).astype(np.uint16)


def unstriped(offs):
    return offs[:16].T.reshape(-1).astype(np.int64)


def pack_weight(w):
    k, n = w.shape
    w = f64(np.asarray(w, np.float32).astype(ml_dtypes.bfloat16)).reshape(k // 32, 32, n)
    amax = np.abs(w).max(1)
    byte = np.clip(np.where(amax > 0, np.frexp(amax)[1] - 1 + 127 - 7, 1), 1, 254)
    scaled = (w * np.exp2(127.0 - byte)[:, None, :]).reshape(k, n).astype(np.float32)
    words = np.ascontiguousarray(scaled.reshape(k // 512, 128, 4, n).transpose(0, 1, 3, 2)).astype(ml_dtypes.float8_e4m3fn).view(np.uint8)
    return words, np.ascontiguousarray(byte.astype(np.uint8).reshape(k // 512, 16, n))


def unpack_weight(words, scales):
    g, p, n, _ = words.shape
    vals = np.ascontiguousarray(words).view(ml_dtypes.float8_e4m3fn).astype(np.float64) * np.repeat(np.exp2(scales.astype(np.float64) - 127.0), 8, axis=1)[..., None]
    return vals.transpose(0, 1, 3, 2).reshape(g * 512, n)


E2M1 = np.array([0.0, 0.5, 1.0, 1.5, 2.0, 3.0, 4.0, 6.0, -0.0, -0.5, -1.0, -1.5, -2.0, -3.0, -4.0, -6.0])


def pack_fp4(w):
    k, n = w.shape
    w = f64(np.asarray(w, np.float32).astype(ml_dtypes.bfloat16)).reshape(k // 32, 32, n)
    amax = np.abs(w).max(1)
    mant, ex = np.frexp(amax / 6.0)
    byte = np.clip(np.where(amax > 0, np.where(mant > 0.5, ex, ex - 1) + 127, 1), 1, 254)
    scaled = (w * np.exp2(127.0 - byte)[:, None, :]).reshape(k, n).astype(np.float32)
    c = np.ascontiguousarray(scaled.reshape(k // 512, 128, 4, n).transpose(0, 1, 3, 2)).astype(ml_dtypes.float4_e2m1fn).view(np.uint8) & 0xF
    words = (c[..., 0::2] | (c[..., 1::2] << 4)).reshape(k // 512, 128, 2 * n)
    return np.ascontiguousarray(words), np.ascontiguousarray(byte.astype(np.uint8).reshape(k // 512, 16, n))


def unpack_fp4(words, scales):
    g, _, n = scales.shape
    words = np.ascontiguousarray(words).reshape(g, 128, n, 2)
    nib = np.empty((g, 128, n, 4), np.uint8)
    nib[..., 0::2] = words & 0xF
    nib[..., 1::2] = words >> 4
    vals = E2M1[nib] * np.repeat(np.exp2(scales.astype(np.float64) - 127.0), 8, axis=1)[..., None]
    return vals.transpose(0, 1, 3, 2).reshape(g * 512, n)


def gelu(v):
    return 0.5 * v * (1.0 + np.tanh(np.sqrt(2.0 / np.pi) * (v + 0.044715 * v**3)))


K, T, S, H, N = 1024, 2048, 512, 512, 256


def setup_inputs():
    n = np.random.standard_normal
    s = mx_kscale(K)[:, None]
    u = mx_kscale(H)
    packed_xT = pack_weight(n((K, T)) * s)
    packed_w2 = pack_fp4(n((H, N)) / np.sqrt(H) / u[:, None])
    return {
        "x_words": packed_xT[0],
        "x_scales": packed_xT[1],
        "w1": (n((K, H)) / np.sqrt(K) / s * u).astype(np.float32),
        "w2_words": packed_w2[0],
        "w2_scales": packed_w2[1],
        "pe": (0.5 * n((H, T)) * u[:, None]).astype(np.float32),
        "offs": striped(np.random.permutation(T)[:S]),
    }


def reference(x_words, x_scales, w1, w2_words, w2_scales, pe, offs):
    xq = unpack_weight(x_words, x_scales)[:, unstriped(offs)]
    g = f64(pe)[:, unstriped(offs)]
    h = gelu((mxq(f64(w1), 0, "e4m3").T @ xq) + g)
    return unpack_fp4(w2_words, w2_scales).T @ mxq(h, 0, "e4m3")

@@ -1,0 +1,153 @@
+from contextlib import ExitStack
+
+import concourse.mybir as mybir
+
+K, T, S, H, N = 1024, 2048, 512, 512, 256
+FLOPS = 2 * K * H * S + 2 * H * N * S
+
+F32 = mybir.dt.float32
+BF16 = mybir.dt.bfloat16
+I32 = mybir.dt.int32
+U32 = mybir.dt.uint32
+U16 = mybir.dt.uint16
+U8 = mybir.dt.uint8
+FP8X4 = mybir.dt.float8_e4m3fn_x4
+FP4X4 = mybir.dt.float4_e2m1fn_x4
+GELU = mybir.ActivationFunctionType.Gelu_apprx_tanh
+ADD = mybir.AluOpType.add
+
+P = 128
+PACK = 4
+PASSES = K // (P * PACK)
+QUADS = 4
+CHUNK = 128
+CHUNKS = S // CHUNK
+M_TILES = N // P
+
+
+def tile_picked_posadd_gelu_p_kernel(tc, x_words, x_scales, w1, w2_words, w2_scales, pe, offs, out):
+    nc = tc.nc
+    with ExitStack() as ctx:
+        held = ctx.enter_context(tc.tile_pool(name="held", bufs=1))
+        psum = ctx.enter_context(tc.psum_pool(name="psum", bufs=1))
+
+        offsets = held.tile([P, S // 16], U16, name="offsets")
+        w1_raw = [held.tile([P, PACK, H], F32, name=f"w1_raw{z}") for z in range(PASSES)]
+        x_table = [held.tile([P, T], I32, name=f"x_table{z}") for z in range(PASSES)]
+        pe_table = [held.tile([P, T], F32, name=f"pe_table{t}") for t in range(PACK)]
+        xs_table = held.tile([P, T], U8, name="xs_table")
+        w2_codes = held.tile([P, 2 * N], U8, name="w2_codes", align_bytes=64)
+        w2_bytes = held.tile([P, N], U8, name="w2_bytes", align_bytes=64)
+
+        nc.vector.memset(xs_table[:].bitcast(I32), 0)
+        nc.vector.memset(w2_bytes[:].bitcast(I32), 0)
+
+        pe_rows = pe.rearrange("(p t) c -> t p c", t=PACK)
+
+        def load_w1(z):
+            nc.sync.dma_start(out=w1_raw[z][:], in_=w1[512 * z : 512 * (z + 1), :].rearrange("(p j) c -> p j c", j=PACK))
+
+        def load_x(z):
+            nc.sync.dma_start(out=x_table[z][:], in_=x_words[z].rearrange("p c r -> p (c r)").bitcast(I32))
+
+        def load_xs(z, q):
+            first = 32 * q + 4 * z
+            nc.sync.dma_start(out=xs_table[first : first + 4, :].bitcast(I32), in_=x_scales[z, 4 * q : 4 * q + 4, :].bitcast(I32))
+
+        load_w1(0)
+        for q in range(QUADS):
+            load_xs(0, q)
+        load_w1(1)
+        for q in range(2):
+            load_xs(1, q)
+        load_x(0)
+        for q in range(2, QUADS):
+            load_xs(1, q)
+        nc.sync.dma_start(offsets[:], offs)
+        load_x(1)
+        for t in range(PACK):
+            nc.sync.dma_start(out=pe_table[t][:], in_=pe_rows[t])
+        nc.sync.dma_start(out=w2_codes[:].bitcast(I32), in_=w2_words[0].bitcast(I32))
+        for q in range(QUADS):
+            nc.sync.dma_start(
+                out=w2_bytes[32 * q : 32 * q + 4, :].bitcast(I32),
+                in_=w2_scales[0, 4 * q : 4 * q + 4, :].bitcast(I32),
+            )
+
+        w1_codes = []
+        w1_bytes = []
+        xs_picked = held.tile([P, S], U8, name="xs_picked", align_bytes=64)
+        for z in range(PASSES):
+            grouped = held.tile([P, PACK, P, PACK], BF16, name=f"w1_grouped{z}", align_bytes=64)
+            src = w1_raw[z][:].rearrange("p j (m t) -> p m j t", t=PACK)
+            dst = grouped[:].rearrange("p t m j -> p m j t")
+            nc.vector.tensor_copy(out=dst[:, 0:64], in_=src[:, 0:64])
+            nc.scalar.copy(out=dst[:, 64:128], in_=src[:, 64:128])
+            if z == 1:
+                nc.vector.tensor_copy(xs_picked[:], xs_table[:].indirect(offsets[:]))
+            codes = held.tile([P, H], U32, name=f"w1_codes{z}", align_bytes=64)
+            sbytes = held.tile([P, H], U8, name=f"w1_bytes{z}", align_bytes=64)
+            nc.vector.quantize_mx(out=codes[:].bitcast(FP8X4), scales=sbytes[:], in_=grouped[:].rearrange("p t m j -> p (t m j)"))
+            w1_codes.append(codes)
+            w1_bytes.append(sbytes)
+
+        acc = [psum.tile([P, S], F32, name=f"acc{t}") for t in range(PACK)]
+        for z in range(PASSES):
+            picked = held.tile([P, S], U32, name=f"x_picked{z}", align_bytes=64)
+            nc.vector.tensor_copy(picked[:], x_table[z][:].bitcast(U32).indirect(offsets[:]))
+            for t in range(PACK):
+                cols = slice(t * P, (t + 1) * P)
+                nc.tensor.matmul_mx(
+                    out=acc[t][:],
+                    lhsT=w1_codes[z][:, cols].bitcast(FP8X4),
+                    lhsT_scale=w1_bytes[z][:, cols],
+                    rhs=picked[:].bitcast(FP8X4),
+                    rhs_scale=xs_picked[4 * z : P, :],
+                    start=(z == 0),
+                    stop=(z == PASSES - 1),
+                )
+
+        sums = [held.tile([P, S], F32, name=f"sums{t}") for t in range(PACK)]
+        for t in range(PACK):
+            nc.scalar.copy(out=sums[t][:], in_=acc[t][:])
+
+        pre = [held.tile([P, 2, S], F32, name=f"pre{u}") for u in range(2)]
+        hidden = [held.tile([P, CHUNK, PACK], BF16, name=f"hidden{c}", align_bytes=64) for c in range(CHUNKS)]
+
+        def gelu(u, c):
+            cols = slice(c * CHUNK, (c + 1) * CHUNK)
+            nc.scalar.activation(hidden[c][:, :, 2 * u : 2 * u + 2], pre[u][:, :, cols].rearrange("p t n -> p n t"), GELU)
+
+        for t in range(PACK - 1):
+            nc.vector.tensor_tensor(pre[t // 2][:, t % 2, :], pe_table[t][:].indirect(offsets[:]), sums[t][:], ADD)
+            if t == 1:
+                for c in range(CHUNKS):
+                    gelu(0, c)
+
+        out_rows = out.rearrange("(m p) c -> p m c", p=P)
+        for c in range(CHUNKS):
+            cols = slice(c * CHUNK, (c + 1) * CHUNK)
+            nc.vector.tensor_tensor(pre[1][:, 1, cols], pe_table[3][:].indirect(offsets[:, c * 8 : (c + 1) * 8]), sums[3][:, cols], ADD)
+            gelu(1, c)
+        for c in range(CHUNKS):
+            cols = slice(c * CHUNK, (c + 1) * CHUNK)
+            h_codes = held.tile([P, CHUNK], U32, name=f"h_codes{c}", align_bytes=64)
+            h_bytes = held.tile([P, CHUNK], U8, name=f"h_bytes{c}", align_bytes=64)
+            nc.vector.quantize_mx(out=h_codes[:].bitcast(FP8X4), scales=h_bytes[:], in_=hidden[c][:].rearrange("p n t -> p (n t)"))
+            res = psum.tile([P, M_TILES, CHUNK], F32, name=f"res{c}")
+            for m in range(M_TILES):
+                nc.tensor.matmul_mx(
+                    out=res[:, m, :],
+                    lhsT=w2_codes[:, 2 * m * P : 2 * (m + 1) * P].bitcast(FP4X4),
+                    lhsT_scale=w2_bytes[:, m * P : (m + 1) * P],
+                    rhs=h_codes[:].bitcast(FP8X4),
+                    rhs_scale=h_bytes[:],
+                    start=True,
+                    stop=True,
+                )
+            staged = held.tile([P, M_TILES, CHUNK], F32, name=f"staged{c}")
+            if c == 2:
+                nc.vector.tensor_copy(out=staged[:], in_=res[:])
+            else:
+                nc.scalar.copy(out=staged[:], in_=res[:])
+            nc.sync.dma_start(out=out_rows[:, :, cols], in_=staged[:])

@@ -33,41 +33,30 @@ def tile_picked_posadd_gelu_p_kernel(tc, x_words, x_scales, w1, w2_words, w2_sca
 
         offsets = held.tile([P, S // 16], U16, name="offsets")
         w1_raw = [held.tile([P, PACK, H], F32, name=f"w1_raw{z}") for z in range(PASSES)]
-        x_table = [held.tile([P, T], I32, name=f"x_table{z}") for z in range(PASSES)]
+        x_table = [held.tile([P, T], I32, name=f"x_table{z}", tag=f"x_table{z}", align_bytes=64) for z in range(PASSES)]
         pe_table = [held.tile([P, T], F32, name=f"pe_table{t}") for t in range(PACK)]
-        xs_table = held.tile([P, T], U8, name="xs_table")
+        xs_table = held.tile([P, T], U8, name="xs_table", tag="xs_table", align_bytes=64)
         w2_codes = held.tile([P, 2 * N], U8, name="w2_codes", align_bytes=64)
         w2_bytes = held.tile([P, N], U8, name="w2_bytes", align_bytes=64)
 
-        nc.vector.memset(xs_table[:].bitcast(I32), 0)
+        nc.gpsimd.memset(xs_table[:].bitcast(I32), 0)
         nc.vector.memset(w2_bytes[:].bitcast(I32), 0)
 
         pe_rows = pe.rearrange("(p t) c -> t p c", t=PACK)
-
-        def load_w1(z):
-            nc.sync.dma_start(out=w1_raw[z][:], in_=w1[512 * z : 512 * (z + 1), :].rearrange("(p j) c -> p j c", j=PACK))
-
-        def load_x(z):
-            nc.sync.dma_start(out=x_table[z][:], in_=x_words[z].rearrange("p c r -> p (c r)").bitcast(I32))
-
-        def load_xs(z, q):
-            first = 32 * q + 4 * z
-            nc.sync.dma_start(out=xs_table[first : first + 4, :].bitcast(I32), in_=x_scales[z, 4 * q : 4 * q + 4, :].bitcast(I32))
-
-        load_w1(0)
-        for q in range(QUADS):
-            load_xs(0, q)
-        load_w1(1)
-        for q in range(2):
-            load_xs(1, q)
-        load_x(0)
-        for q in range(2, QUADS):
-            load_xs(1, q)
+        nc.sync.dma_start(out=w1_raw[0][:], in_=w1[0:512, :].rearrange("(p j) c -> p j c", j=PACK))
         nc.sync.dma_start(offsets[:], offs)
-        load_x(1)
+        nc.sync.dma_start(out=w1_raw[1][:], in_=w1[512:1024, :].rearrange("(p j) c -> p j c", j=PACK))
+        for z in range(PASSES):
+            nc.sync.dma_start(out=x_table[z][:], in_=x_words[z].rearrange("p c r -> p (c r)").bitcast(I32))
         for t in range(PACK):
             nc.sync.dma_start(out=pe_table[t][:], in_=pe_rows[t])
         nc.sync.dma_start(out=w2_codes[:].bitcast(I32), in_=w2_words[0].bitcast(I32))
+
+        for q in range(QUADS):
+            nc.gpsimd.dma_start(
+                out=xs_table[32 * q : 32 * q + 4 * PASSES, :].bitcast(I32),
+                in_=x_scales[:, 4 * q : 4 * q + 4, :].bitcast(I32),
+            )
         for q in range(QUADS):
             nc.sync.dma_start(
                 out=w2_bytes[32 * q : 32 * q + 4, :].bitcast(I32),
@@ -91,9 +80,9 @@ def tile_picked_posadd_gelu_p_kernel(tc, x_words, x_scales, w1, w2_words, w2_sca
             w1_codes.append(codes)
             w1_bytes.append(sbytes)
 
-        acc = [psum.tile([P, S], F32, name=f"acc{t}") for t in range(PACK)]
+        acc = [psum.tile([P, S], F32, name=f"acc{t}", tag=f"acc{t}") for t in range(PACK)]
         for z in range(PASSES):
-            picked = held.tile([P, S], U32, name=f"x_picked{z}", align_bytes=64)
+            picked = held.tile([P, S], U32, name=f"x_picked{z}", tag=("xs_table", "x_table0")[z], align_bytes=64)
             nc.vector.tensor_copy(picked[:], x_table[z][:].bitcast(U32).indirect(offsets[:]))
             for t in range(PACK):
                 cols = slice(t * P, (t + 1) * P)
@@ -114,30 +103,33 @@ def tile_picked_posadd_gelu_p_kernel(tc, x_words, x_scales, w1, w2_words, w2_sca
         pre = [held.tile([P, 2, S], F32, name=f"pre{u}") for u in range(2)]
         hidden = [held.tile([P, CHUNK, PACK], BF16, name=f"hidden{c}", align_bytes=64) for c in range(CHUNKS)]
 
-        def gelu(u, c):
-            cols = slice(c * CHUNK, (c + 1) * CHUNK)
-            nc.scalar.activation(hidden[c][:, :, 2 * u : 2 * u + 2], pre[u][:, :, cols].rearrange("p t n -> p n t"), GELU)
+        def gelu(u, c, lo, hi):
+            cols = slice(c * CHUNK + lo, c * CHUNK + hi)
+            nc.scalar.activation(hidden[c][:, lo:hi, 2 * u : 2 * u + 2], pre[u][:, :, cols].rearrange("p t n -> p n t"), GELU)
 
         for t in range(PACK - 1):
             nc.vector.tensor_tensor(pre[t // 2][:, t % 2, :], pe_table[t][:].indirect(offsets[:]), sums[t][:], ADD)
             if t == 1:
                 for c in range(CHUNKS):
-                    gelu(0, c)
+                    gelu(0, c, 0, CHUNK)
 
         out_rows = out.rearrange("(m p) c -> p m c", p=P)
         for c in range(CHUNKS):
-            cols = slice(c * CHUNK, (c + 1) * CHUNK)
-            nc.vector.tensor_tensor(pre[1][:, 1, cols], pe_table[3][:].indirect(offsets[:, c * 8 : (c + 1) * 8]), sums[3][:, cols], ADD)
-            gelu(1, c)
+            for lo, hi in ((0, 64), (64, CHUNK)) if c == 0 else ((0, CHUNK),):
+                first, last = c * CHUNK + lo, c * CHUNK + hi
+                nc.vector.tensor_tensor(
+                    pre[1][:, 1, first:last], pe_table[3][:].indirect(offsets[:, first // 16 : last // 16]), sums[3][:, first:last], ADD
+                )
+                gelu(1, c, lo, hi)
         for c in range(CHUNKS):
             cols = slice(c * CHUNK, (c + 1) * CHUNK)
             h_codes = held.tile([P, CHUNK], U32, name=f"h_codes{c}", align_bytes=64)
             h_bytes = held.tile([P, CHUNK], U8, name=f"h_bytes{c}", align_bytes=64)
             nc.vector.quantize_mx(out=h_codes[:].bitcast(FP8X4), scales=h_bytes[:], in_=hidden[c][:].rearrange("p n t -> p (n t)"))
-            res = psum.tile([P, M_TILES, CHUNK], F32, name=f"res{c}")
-            for m in range(M_TILES):
+
+            def product(res, m):
                 nc.tensor.matmul_mx(
-                    out=res[:, m, :],
+                    out=res,
                     lhsT=w2_codes[:, 2 * m * P : 2 * (m + 1) * P].bitcast(FP4X4),
                     lhsT_scale=w2_bytes[:, m * P : (m + 1) * P],
                     rhs=h_codes[:].bitcast(FP8X4),
@@ -145,9 +137,25 @@ def tile_picked_posadd_gelu_p_kernel(tc, x_words, x_scales, w1, w2_words, w2_sca
                     start=True,
                     stop=True,
                 )
-            staged = held.tile([P, M_TILES, CHUNK], F32, name=f"staged{c}")
-            if c == 2:
-                nc.vector.tensor_copy(out=staged[:], in_=res[:])
+
+            if c < CHUNKS - 1:
+                res = psum.tile([P, M_TILES, CHUNK], F32, name=f"res{c}")
+                for m in range(M_TILES):
+                    product(res[:, m, :], m)
+                staged = held.tile([P, M_TILES, CHUNK], F32, name=f"staged{c}")
+                if c == 2:
+                    nc.vector.tensor_copy(out=staged[:], in_=res[:])
+                else:
+                    nc.scalar.copy(out=staged[:], in_=res[:])
+                nc.sync.dma_start(out=out_rows[:, :, cols], in_=staged[:])
             else:
-                nc.scalar.copy(out=staged[:], in_=res[:])
-            nc.sync.dma_start(out=out_rows[:, :, cols], in_=staged[:])
+                for m in range(M_TILES):
+                    res = psum.tile([P, CHUNK], F32, name=f"last{m}", tag=("last", "acc0")[m])
+                    product(res[:], m)
+                    staged = held.tile([P, CHUNK], F32, name=f"staged_last{m}")
+                    if m == 0:
+                        nc.scalar.copy(out=staged[:], in_=res[:])
+                        nc.scalar.dma_start(out=out_rows[:, m, cols], in_=staged[:])
+                    else:
+                        nc.vector.tensor_copy(out=staged[:], in_=res[:])
+                        nc.sync.dma_start(out=out_rows[:, m, cols], in_=staged[:])

@@ -39,57 +39,61 @@ def tile_picked_posadd_gelu_p_kernel(tc, x_words, x_scales, w1, w2_words, w2_sca
         w2_codes = held.tile([P, 2 * N], U8, name="w2_codes", align_bytes=64)
         w2_bytes = held.tile([P, N], U8, name="w2_bytes", align_bytes=64)
 
-        nc.gpsimd.memset(xs_table[:].bitcast(I32), 0)
+        nc.vector.memset(xs_table[:].bitcast(I32), 0)
         nc.vector.memset(w2_bytes[:].bitcast(I32), 0)
 
         pe_rows = pe.rearrange("(p t) c -> t p c", t=PACK)
-        nc.sync.dma_start(out=w1_raw[0][:], in_=w1[0:512, :].rearrange("(p j) c -> p j c", j=PACK))
-        nc.sync.dma_start(offsets[:], offs)
-        nc.sync.dma_start(out=w1_raw[1][:], in_=w1[512:1024, :].rearrange("(p j) c -> p j c", j=PACK))
-        for z in range(PASSES):
-            nc.sync.dma_start(out=x_table[z][:], in_=x_words[z].rearrange("p c r -> p (c r)").bitcast(I32))
-        for t in range(PACK):
-            nc.sync.dma_start(out=pe_table[t][:], in_=pe_rows[t])
-        nc.sync.dma_start(out=w2_codes[:].bitcast(I32), in_=w2_words[0].bitcast(I32))
 
+        def load_w1(z):
+            nc.sync.dma_start(out=w1_raw[z][:], in_=w1[512 * z : 512 * (z + 1), :].rearrange("(p j) c -> p j c", j=PACK))
+
+        def load_x(z):
+            nc.sync.dma_start(out=x_table[z][:], in_=x_words[z].rearrange("p c r -> p (c r)").bitcast(I32))
+
+        load_w1(0)
         for q in range(QUADS):
-            nc.gpsimd.dma_start(
+            nc.sync.dma_start(
                 out=xs_table[32 * q : 32 * q + 4 * PASSES, :].bitcast(I32),
                 in_=x_scales[:, 4 * q : 4 * q + 4, :].bitcast(I32),
             )
+        nc.sync.dma_start(offsets[:], offs)
+        load_x(0)
+        load_w1(1)
+        load_x(1)
+        for t in range(PACK):
+            nc.sync.dma_start(out=pe_table[t][:], in_=pe_rows[t])
+        nc.sync.dma_start(out=w2_codes[:].bitcast(I32), in_=w2_words[0].bitcast(I32))
         for q in range(QUADS):
             nc.sync.dma_start(
                 out=w2_bytes[32 * q : 32 * q + 4, :].bitcast(I32),
                 in_=w2_scales[0, 4 * q : 4 * q + 4, :].bitcast(I32),
             )
 
-        w1_codes = []
-        w1_bytes = []
+        warm = held.tile([P, 2], F32, name="warm")
+        nc.vector.memset(warm[:, 0:1], 0.0)
+        nc.scalar.activation(warm[:, 1:2], warm[:, 0:1], GELU)
+
         xs_picked = held.tile([P, S], U8, name="xs_picked", align_bytes=64)
+        acc = [psum.tile([P, S], F32, name=f"acc{t}", tag=f"acc{t}") for t in range(PACK)]
         for z in range(PASSES):
             grouped = held.tile([P, PACK, P, PACK], BF16, name=f"w1_grouped{z}", align_bytes=64)
             src = w1_raw[z][:].rearrange("p j (m t) -> p m j t", t=PACK)
             dst = grouped[:].rearrange("p t m j -> p m j t")
             nc.vector.tensor_copy(out=dst[:, 0:64], in_=src[:, 0:64])
             nc.scalar.copy(out=dst[:, 64:128], in_=src[:, 64:128])
-            if z == 1:
+            if z == 0:
                 nc.vector.tensor_copy(xs_picked[:], xs_table[:].indirect(offsets[:]))
             codes = held.tile([P, H], U32, name=f"w1_codes{z}", align_bytes=64)
             sbytes = held.tile([P, H], U8, name=f"w1_bytes{z}", align_bytes=64)
             nc.vector.quantize_mx(out=codes[:].bitcast(FP8X4), scales=sbytes[:], in_=grouped[:].rearrange("p t m j -> p (t m j)"))
-            w1_codes.append(codes)
-            w1_bytes.append(sbytes)
-
-        acc = [psum.tile([P, S], F32, name=f"acc{t}", tag=f"acc{t}") for t in range(PACK)]
-        for z in range(PASSES):
-            picked = held.tile([P, S], U32, name=f"x_picked{z}", tag=("xs_table", "x_table0")[z], align_bytes=64)
+            picked = held.tile([P, S], U32, name=f"x_picked{z}", align_bytes=64)
             nc.vector.tensor_copy(picked[:], x_table[z][:].bitcast(U32).indirect(offsets[:]))
             for t in range(PACK):
                 cols = slice(t * P, (t + 1) * P)
                 nc.tensor.matmul_mx(
                     out=acc[t][:],
-                    lhsT=w1_codes[z][:, cols].bitcast(FP8X4),
-                    lhsT_scale=w1_bytes[z][:, cols],
+                    lhsT=codes[:, cols].bitcast(FP8X4),
+                    lhsT_scale=sbytes[:, cols],
                     rhs=picked[:].bitcast(FP8X4),
                     rhs_scale=xs_picked[4 * z : P, :],
                     start=(z == 0),

@@ -77,10 +77,9 @@ def tile_picked_posadd_gelu_p_kernel(tc, x_words, x_scales, w1, w2_words, w2_sca
         acc = [psum.tile([P, S], F32, name=f"acc{t}", tag=f"acc{t}") for t in range(PACK)]
         for z in range(PASSES):
             grouped = held.tile([P, PACK, P, PACK], BF16, name=f"w1_grouped{z}", align_bytes=64)
-            src = w1_raw[z][:].rearrange("p j (m t) -> p m j t", t=PACK)
-            dst = grouped[:].rearrange("p t m j -> p m j t")
-            nc.vector.tensor_copy(out=dst[:, 0:64], in_=src[:, 0:64])
-            nc.scalar.copy(out=dst[:, 64:128], in_=src[:, 64:128])
+            src = w1_raw[z][:].rearrange("p j (m t) -> p t m j", t=PACK)
+            nc.vector.tensor_copy(out=grouped[:, 0:2], in_=src[:, 0:2])
+            nc.scalar.copy(out=grouped[:, 2:4], in_=src[:, 2:4])
             if z == 0:
                 nc.vector.tensor_copy(xs_picked[:], xs_table[:].indirect(offsets[:]))
             codes = held.tile([P, H], U32, name=f"w1_codes{z}", align_bytes=64)

@@ -18,11 +18,17 @@ ADD = mybir.AluOpType.add
 
 P = 128
 PACK = 4
-PASSES = K // (P * PACK)
+K_PASS = P * PACK
+PASSES = K // K_PASS
 QUADS = 4
+QUAD = P // QUADS
+ROWS = 4
+LIST_COL = 16
+PAIR = 2
 CHUNK = 128
 CHUNKS = S // CHUNK
 M_TILES = N // P
+ALIGN = 64
 
 
 def tile_picked_posadd_gelu_p_kernel(tc, x_words, x_scales, w1, w2_words, w2_scales, pe, offs, out):
@@ -31,21 +37,20 @@ def tile_picked_posadd_gelu_p_kernel(tc, x_words, x_scales, w1, w2_words, w2_sca
         held = ctx.enter_context(tc.tile_pool(name="held", bufs=1))
         psum = ctx.enter_context(tc.psum_pool(name="psum", bufs=1))
 
-        offsets = held.tile([P, S // 16], U16, name="offsets")
+        offsets = held.tile([P, S // LIST_COL], U16, name="offsets")
         w1_raw = [held.tile([P, PACK, H], F32, name=f"w1_raw{z}") for z in range(PASSES)]
-        x_table = [held.tile([P, T], I32, name=f"x_table{z}", tag=f"x_table{z}", align_bytes=64) for z in range(PASSES)]
+        x_table = [held.tile([P, T], I32, name=f"x_table{z}", align_bytes=ALIGN) for z in range(PASSES)]
         pe_table = [held.tile([P, T], F32, name=f"pe_table{t}") for t in range(PACK)]
-        xs_table = held.tile([P, T], U8, name="xs_table", tag="xs_table", align_bytes=64)
-        w2_codes = held.tile([P, 2 * N], U8, name="w2_codes", align_bytes=64)
-        w2_bytes = held.tile([P, N], U8, name="w2_bytes", align_bytes=64)
+        xs_table = held.tile([P, T], U8, name="xs_table", align_bytes=ALIGN)
+        w2_codes = held.tile([P, 2 * N], U8, name="w2_codes", align_bytes=ALIGN)
+        w2_bytes = held.tile([P, N], U8, name="w2_bytes", align_bytes=ALIGN)
 
         nc.vector.memset(xs_table[:].bitcast(I32), 0)
         nc.vector.memset(w2_bytes[:].bitcast(I32), 0)
 
-        pe_rows = pe.rearrange("(p t) c -> t p c", t=PACK)
-
         def load_w1(z):
-            nc.sync.dma_start(out=w1_raw[z][:], in_=w1[512 * z : 512 * (z + 1), :].rearrange("(p j) c -> p j c", j=PACK))
+            rows = w1[K_PASS * z : K_PASS * (z + 1), :]
+            nc.sync.dma_start(out=w1_raw[z][:], in_=rows.rearrange("(p j) c -> p j c", j=PACK))
 
         def load_x(z):
             nc.sync.dma_start(out=x_table[z][:], in_=x_words[z].rearrange("p c r -> p (c r)").bitcast(I32))
@@ -53,48 +58,47 @@ def tile_picked_posadd_gelu_p_kernel(tc, x_words, x_scales, w1, w2_words, w2_sca
         load_w1(0)
         for q in range(QUADS):
             nc.sync.dma_start(
-                out=xs_table[32 * q : 32 * q + 4 * PASSES, :].bitcast(I32),
-                in_=x_scales[:, 4 * q : 4 * q + 4, :].bitcast(I32),
+                out=xs_table[QUAD * q : QUAD * q + ROWS * PASSES, :].bitcast(I32),
+                in_=x_scales[:, ROWS * q : ROWS * (q + 1), :].bitcast(I32),
             )
         nc.sync.dma_start(offsets[:], offs)
         load_x(0)
         load_w1(1)
         load_x(1)
+        pe_rows = pe.rearrange("(p t) c -> t p c", t=PACK)
         for t in range(PACK):
             nc.sync.dma_start(out=pe_table[t][:], in_=pe_rows[t])
         nc.sync.dma_start(out=w2_codes[:].bitcast(I32), in_=w2_words[0].bitcast(I32))
         for q in range(QUADS):
             nc.sync.dma_start(
-                out=w2_bytes[32 * q : 32 * q + 4, :].bitcast(I32),
-                in_=w2_scales[0, 4 * q : 4 * q + 4, :].bitcast(I32),
+                out=w2_bytes[QUAD * q : QUAD * q + ROWS, :].bitcast(I32),
+                in_=w2_scales[0, ROWS * q : ROWS * (q + 1), :].bitcast(I32),
             )
 
-        warm = held.tile([P, 2], F32, name="warm")
-        nc.vector.memset(warm[:, 0:1], 0.0)
-        nc.scalar.activation(warm[:, 1:2], warm[:, 0:1], GELU)
-
-        xs_picked = held.tile([P, S], U8, name="xs_picked", align_bytes=64)
+        xs_picked = held.tile([P, S], U8, name="xs_picked", align_bytes=ALIGN)
         acc = [psum.tile([P, S], F32, name=f"acc{t}", tag=f"acc{t}") for t in range(PACK)]
         for z in range(PASSES):
-            grouped = held.tile([P, PACK, P, PACK], BF16, name=f"w1_grouped{z}", align_bytes=64)
-            src = w1_raw[z][:].rearrange("p j (m t) -> p t m j", t=PACK)
-            nc.vector.tensor_copy(out=grouped[:, 0:2], in_=src[:, 0:2])
-            nc.scalar.copy(out=grouped[:, 2:4], in_=src[:, 2:4])
+            grouped = held.tile([P, PACK, P, PACK], BF16, name=f"w1_grouped{z}", align_bytes=ALIGN)
+            dealt = w1_raw[z][:].rearrange("p j (m t) -> p t m j", t=PACK)
+            nc.vector.tensor_copy(out=grouped[:, : PACK // 2], in_=dealt[:, : PACK // 2])
+            nc.scalar.copy(out=grouped[:, PACK // 2 :], in_=dealt[:, PACK // 2 :])
             if z == 0:
                 nc.vector.tensor_copy(xs_picked[:], xs_table[:].indirect(offsets[:]))
-            codes = held.tile([P, H], U32, name=f"w1_codes{z}", align_bytes=64)
-            sbytes = held.tile([P, H], U8, name=f"w1_bytes{z}", align_bytes=64)
-            nc.vector.quantize_mx(out=codes[:].bitcast(FP8X4), scales=sbytes[:], in_=grouped[:].rearrange("p t m j -> p (t m j)"))
-            picked = held.tile([P, S], U32, name=f"x_picked{z}", align_bytes=64)
-            nc.vector.tensor_copy(picked[:], x_table[z][:].bitcast(U32).indirect(offsets[:]))
+            w1_codes = held.tile([P, H], U32, name=f"w1_codes{z}", align_bytes=ALIGN)
+            w1_bytes = held.tile([P, H], U8, name=f"w1_bytes{z}", align_bytes=ALIGN)
+            nc.vector.quantize_mx(
+                out=w1_codes[:].bitcast(FP8X4), scales=w1_bytes[:], in_=grouped[:].rearrange("p t m j -> p (t m j)")
+            )
+            x_picked = held.tile([P, S], U32, name=f"x_picked{z}", align_bytes=ALIGN)
+            nc.vector.tensor_copy(x_picked[:], x_table[z][:].bitcast(U32).indirect(offsets[:]))
             for t in range(PACK):
-                cols = slice(t * P, (t + 1) * P)
+                group = slice(t * P, (t + 1) * P)
                 nc.tensor.matmul_mx(
                     out=acc[t][:],
-                    lhsT=codes[:, cols].bitcast(FP8X4),
-                    lhsT_scale=sbytes[:, cols],
-                    rhs=picked[:].bitcast(FP8X4),
-                    rhs_scale=xs_picked[4 * z : P, :],
+                    lhsT=w1_codes[:, group].bitcast(FP8X4),
+                    lhsT_scale=w1_bytes[:, group],
+                    rhs=x_picked[:].bitcast(FP8X4),
+                    rhs_scale=xs_picked[ROWS * z : P, :],
                     start=(z == 0),
                     stop=(z == PASSES - 1),
                 )
@@ -103,62 +107,68 @@ def tile_picked_posadd_gelu_p_kernel(tc, x_words, x_scales, w1, w2_words, w2_sca
         for t in range(PACK):
             nc.scalar.copy(out=sums[t][:], in_=acc[t][:])
 
-        pre = [held.tile([P, 2, S], F32, name=f"pre{u}") for u in range(2)]
-        hidden = [held.tile([P, CHUNK, PACK], BF16, name=f"hidden{c}", align_bytes=64) for c in range(CHUNKS)]
+        pre = [held.tile([P, PAIR, S], F32, name=f"pre{u}") for u in range(PACK // PAIR)]
+        hidden = [held.tile([P, CHUNK, PACK], BF16, name=f"hidden{c}", align_bytes=ALIGN) for c in range(CHUNKS)]
 
-        def gelu(u, c, lo, hi):
-            cols = slice(c * CHUNK + lo, c * CHUNK + hi)
-            nc.scalar.activation(hidden[c][:, lo:hi, 2 * u : 2 * u + 2], pre[u][:, :, cols].rearrange("p t n -> p n t"), GELU)
+        def add_pe(t, first, last):
+            entries = offsets[:, first // LIST_COL : last // LIST_COL]
+            nc.vector.tensor_tensor(pre[t // PAIR][:, t % PAIR, first:last], pe_table[t][:].indirect(entries), sums[t][:, first:last], ADD)
 
-        for t in range(PACK - 1):
-            nc.vector.tensor_tensor(pre[t // 2][:, t % 2, :], pe_table[t][:].indirect(offsets[:]), sums[t][:], ADD)
-            if t == 1:
-                for c in range(CHUNKS):
-                    gelu(0, c, 0, CHUNK)
+        def gelu(u, first, last):
+            c, n = divmod(first, CHUNK)
+            nc.scalar.activation(
+                hidden[c][:, n : n + last - first, PAIR * u : PAIR * (u + 1)],
+                pre[u][:, :, first:last].rearrange("p e j -> p j e"),
+                GELU,
+            )
 
-        out_rows = out.rearrange("(m p) c -> p m c", p=P)
+        for t in range(PAIR):
+            add_pe(t, 0, S)
         for c in range(CHUNKS):
-            for lo, hi in ((0, 64), (64, CHUNK)) if c == 0 else ((0, CHUNK),):
-                first, last = c * CHUNK + lo, c * CHUNK + hi
-                nc.vector.tensor_tensor(
-                    pre[1][:, 1, first:last], pe_table[3][:].indirect(offsets[:, first // 16 : last // 16]), sums[3][:, first:last], ADD
-                )
-                gelu(1, c, lo, hi)
-        for c in range(CHUNKS):
-            cols = slice(c * CHUNK, (c + 1) * CHUNK)
-            h_codes = held.tile([P, CHUNK], U32, name=f"h_codes{c}", align_bytes=64)
-            h_bytes = held.tile([P, CHUNK], U8, name=f"h_bytes{c}", align_bytes=64)
+            gelu(0, c * CHUNK, (c + 1) * CHUNK)
+        add_pe(PACK - 2, 0, S)
+
+        cuts = [0, CHUNK // 2] + [c * CHUNK for c in range(1, CHUNKS + 1)]
+        for first, last in zip(cuts[:-1], cuts[1:]):
+            add_pe(PACK - 1, first, last)
+            gelu(1, first, last)
+
+        out_rows = out.rearrange("(m p) j -> p m j", p=P)
+
+        def quantize_hidden(c):
+            h_codes = held.tile([P, CHUNK], U32, name=f"h_codes{c}", align_bytes=ALIGN)
+            h_bytes = held.tile([P, CHUNK], U8, name=f"h_bytes{c}", align_bytes=ALIGN)
             nc.vector.quantize_mx(out=h_codes[:].bitcast(FP8X4), scales=h_bytes[:], in_=hidden[c][:].rearrange("p n t -> p (n t)"))
+            return h_codes, h_bytes
 
-            def product(res, m):
-                nc.tensor.matmul_mx(
-                    out=res,
-                    lhsT=w2_codes[:, 2 * m * P : 2 * (m + 1) * P].bitcast(FP4X4),
-                    lhsT_scale=w2_bytes[:, m * P : (m + 1) * P],
-                    rhs=h_codes[:].bitcast(FP8X4),
-                    rhs_scale=h_bytes[:],
-                    start=True,
-                    stop=True,
-                )
+        def second_product(result, m, h_codes, h_bytes):
+            nc.tensor.matmul_mx(
+                out=result,
+                lhsT=w2_codes[:, 2 * m * P : 2 * (m + 1) * P].bitcast(FP4X4),
+                lhsT_scale=w2_bytes[:, m * P : (m + 1) * P],
+                rhs=h_codes[:].bitcast(FP8X4),
+                rhs_scale=h_bytes[:],
+                start=True,
+                stop=True,
+            )
 
-            if c < CHUNKS - 1:
-                res = psum.tile([P, M_TILES, CHUNK], F32, name=f"res{c}")
-                for m in range(M_TILES):
-                    product(res[:, m, :], m)
-                staged = held.tile([P, M_TILES, CHUNK], F32, name=f"staged{c}")
-                if c == 2:
-                    nc.vector.tensor_copy(out=staged[:], in_=res[:])
-                else:
-                    nc.scalar.copy(out=staged[:], in_=res[:])
-                nc.sync.dma_start(out=out_rows[:, :, cols], in_=staged[:])
+        for c in range(CHUNKS - 1):
+            h_codes, h_bytes = quantize_hidden(c)
+            res = psum.tile([P, M_TILES, CHUNK], F32, name=f"res{c}")
+            for m in range(M_TILES):
+                second_product(res[:, m, :], m, h_codes, h_bytes)
+            staged = held.tile([P, M_TILES, CHUNK], F32, name=f"staged{c}")
+            if c == CHUNKS - 2:
+                nc.vector.tensor_copy(out=staged[:], in_=res[:])
             else:
-                for m in range(M_TILES):
-                    res = psum.tile([P, CHUNK], F32, name=f"last{m}", tag=("last", "acc0")[m])
-                    product(res[:], m)
-                    staged = held.tile([P, CHUNK], F32, name=f"staged_last{m}")
-                    if m == 0:
-                        nc.scalar.copy(out=staged[:], in_=res[:])
-                        nc.scalar.dma_start(out=out_rows[:, m, cols], in_=staged[:])
-                    else:
-                        nc.vector.tensor_copy(out=staged[:], in_=res[:])
-                        nc.sync.dma_start(out=out_rows[:, m, cols], in_=staged[:])
+                nc.scalar.copy(out=staged[:], in_=res[:])
+            nc.sync.dma_start(out=out_rows[:, :, c * CHUNK : (c + 1) * CHUNK], in_=staged[:])
+
+        h_codes, h_bytes = quantize_hidden(CHUNKS - 1)
+        ways_out = (("last", nc.scalar.copy, nc.scalar), ("acc0", nc.vector.tensor_copy, nc.sync))
+        for m, (bank, copy_out, queue) in enumerate(ways_out):
+            res = psum.tile([P, CHUNK], F32, name=f"last{m}", tag=bank)
+            second_product(res[:], m, h_codes, h_bytes)
+            staged = held.tile([P, CHUNK], F32, name=f"staged_last{m}")
+            copy_out(out=staged[:], in_=res[:])
+            queue.dma_start(out=out_rows[:, m, S - CHUNK : S], in_=staged[:])

@@ -28,6 +28,8 @@ PAIR = 2
 CHUNK = 128
 CHUNKS = S // CHUNK
 M_TILES = N // P
+SPREAD_FROM, SPREAD = 32, 4
+TABLE = 4 * T
 ALIGN = 64
 
 
@@ -35,18 +37,23 @@ def tile_picked_posadd_gelu_p_kernel(tc, x_words, x_scales, w1, w2_words, w2_sca
     nc = tc.nc
     with ExitStack() as ctx:
         held = ctx.enter_context(tc.tile_pool(name="held", bufs=1))
+        shared = ctx.enter_context(tc.tile_pool(name="shared", bufs=1))
         psum = ctx.enter_context(tc.psum_pool(name="psum", bufs=1))
 
         offsets = held.tile([P, S // LIST_COL], U16, name="offsets")
         w1_raw = [held.tile([P, PACK, H], F32, name=f"w1_raw{z}") for z in range(PASSES)]
         x_table = [held.tile([P, T], I32, name=f"x_table{z}", align_bytes=ALIGN) for z in range(PASSES)]
-        pe_table = [held.tile([P, T], F32, name=f"pe_table{t}") for t in range(PACK)]
-        xs_table = held.tile([P, T], U8, name="xs_table", align_bytes=ALIGN)
-        w2_codes = held.tile([P, 2 * N], U8, name="w2_codes", align_bytes=ALIGN)
-        w2_bytes = held.tile([P, N], U8, name="w2_bytes", align_bytes=ALIGN)
+        xs_table = shared.tile([P, PASSES, T], U8, name="xs_table", offset=TABLE - T)
+        xs_plane = held.tile([P, PASSES, S], U8, name="xs_plane", align_bytes=ALIGN)
 
-        nc.vector.memset(xs_table[:].bitcast(I32), 0)
-        nc.vector.memset(w2_bytes[:].bitcast(I32), 0)
+        nc.vector.memset(xs_table[:].rearrange("p z c -> p (z c)").bitcast(I32), 0)
+        nc.vector.memset(xs_plane[:].rearrange("p z c -> p (z c)").bitcast(I32), 0)
+        pe_rows = pe.rearrange("(p t) c -> t p c", t=PACK)
+        pe_table = []
+
+        def load_pe(t):
+            pe_table.append(shared.tile([P, T], F32, name=f"pe_table{t}", offset=t * TABLE))
+            nc.sync.dma_start(out=pe_table[t][:], in_=pe_rows[t])
 
         def load_w1(z):
             rows = w1[K_PASS * z : K_PASS * (z + 1), :]
@@ -56,36 +63,35 @@ def tile_picked_posadd_gelu_p_kernel(tc, x_words, x_scales, w1, w2_words, w2_sca
             nc.sync.dma_start(out=x_table[z][:], in_=x_words[z].rearrange("p c r -> p (c r)").bitcast(I32))
 
         load_w1(0)
-        for q in range(QUADS):
-            nc.sync.dma_start(
-                out=xs_table[QUAD * q : QUAD * q + ROWS * PASSES, :].bitcast(I32),
-                in_=x_scales[:, ROWS * q : ROWS * (q + 1), :].bitcast(I32),
-            )
+        nc.sync.dma_start(
+            out=xs_table[SPREAD_FROM : SPREAD_FROM + SPREAD * QUADS * ROWS : SPREAD].bitcast(I32),
+            in_=x_scales.rearrange("z r c -> r z c").bitcast(I32),
+        )
         nc.sync.dma_start(offsets[:], offs)
         load_x(0)
         load_w1(1)
         load_x(1)
-        pe_rows = pe.rearrange("(p t) c -> t p c", t=PACK)
-        for t in range(PACK):
-            nc.sync.dma_start(out=pe_table[t][:], in_=pe_rows[t])
-        nc.sync.dma_start(out=w2_codes[:].bitcast(I32), in_=w2_words[0].bitcast(I32))
-        for q in range(QUADS):
-            nc.sync.dma_start(
-                out=w2_bytes[QUAD * q : QUAD * q + ROWS, :].bitcast(I32),
-                in_=w2_scales[0, ROWS * q : ROWS * (q + 1), :].bitcast(I32),
-            )
 
-        xs_picked = held.tile([P, S], U8, name="xs_picked", align_bytes=ALIGN)
+        xs_picked = shared.tile([P, PASSES, S], U8, name="xs_picked", offset=3 * TABLE - S)
+        for z in range(PASSES):
+            nc.vector.tensor_copy(xs_picked[:, z, :], xs_table[:, z, :].indirect(offsets[:]))
+        for q in range(QUADS):
+            first = SPREAD_FROM + SPREAD * ROWS * q
+            nc.sync.dma_start(
+                out=xs_plane[QUAD * q : QUAD * q + ROWS].rearrange("p z c -> p (z c)").bitcast(I32),
+                in_=xs_picked[first : first + SPREAD * ROWS : SPREAD].rearrange("p z c -> p (z c)").bitcast(I32),
+            )
+        for t in range(PACK):
+            load_pe(t)
+
         acc = [psum.tile([P, S], F32, name=f"acc{t}", tag=f"acc{t}") for t in range(PACK)]
         for z in range(PASSES):
             grouped = held.tile([P, PACK, P, PACK], BF16, name=f"w1_grouped{z}", align_bytes=ALIGN)
             dealt = w1_raw[z][:].rearrange("p j (m t) -> p t m j", t=PACK)
             nc.vector.tensor_copy(out=grouped[:, : PACK // 2], in_=dealt[:, : PACK // 2])
             nc.scalar.copy(out=grouped[:, PACK // 2 :], in_=dealt[:, PACK // 2 :])
-            if z == 0:
-                nc.vector.tensor_copy(xs_picked[:], xs_table[:].indirect(offsets[:]))
-            w1_codes = held.tile([P, H], U32, name=f"w1_codes{z}", align_bytes=ALIGN)
-            w1_bytes = held.tile([P, H], U8, name=f"w1_bytes{z}", align_bytes=ALIGN)
+            w1_codes = held.tile([P, H], U32, name=f"w1_codes{z}", tag=f"w1_codes{z}", align_bytes=ALIGN)
+            w1_bytes = held.tile([P, H], U8, name=f"w1_bytes{z}", tag=f"w1_bytes{z}", align_bytes=ALIGN)
             nc.vector.quantize_mx(
                 out=w1_codes[:].bitcast(FP8X4), scales=w1_bytes[:], in_=grouped[:].rearrange("p t m j -> p (t m j)")
             )
@@ -98,10 +104,20 @@ def tile_picked_posadd_gelu_p_kernel(tc, x_words, x_scales, w1, w2_words, w2_sca
                     lhsT=w1_codes[:, group].bitcast(FP8X4),
                     lhsT_scale=w1_bytes[:, group],
                     rhs=x_picked[:].bitcast(FP8X4),
-                    rhs_scale=xs_picked[ROWS * z : P, :],
+                    rhs_scale=xs_plane[:, z, :],
                     start=(z == 0),
                     stop=(z == PASSES - 1),
                 )
+
+        w2_codes = held.tile([P, 2 * N], U8, name="w2_codes", tag="w1_codes0", align_bytes=ALIGN)
+        w2_bytes = held.tile([P, N], U8, name="w2_bytes", tag="w1_bytes0", align_bytes=ALIGN)
+        nc.vector.memset(w2_bytes[:].bitcast(I32), 0)
+        nc.sync.dma_start(out=w2_codes[:].bitcast(I32), in_=w2_words[0].bitcast(I32))
+        for q in range(QUADS):
+            nc.sync.dma_start(
+                out=w2_bytes[QUAD * q : QUAD * q + ROWS, :].bitcast(I32),
+                in_=w2_scales[0, ROWS * q : ROWS * (q + 1), :].bitcast(I32),
+            )
 
         sums = [held.tile([P, S], F32, name=f"sums{t}") for t in range(PACK)]
         for t in range(PACK):

@@ -1,3 +1,4 @@
+import itertools
 from contextlib import ExitStack
 
 import concourse.mybir as mybir
@@ -30,6 +31,7 @@ CHUNKS = S // CHUNK
 M_TILES = N // P
 SPREAD_FROM, SPREAD = 32, 4
 TABLE = 4 * T
+W2_BYTES = 3 * N
 ALIGN = 64
 
 
@@ -52,7 +54,7 @@ def tile_picked_posadd_gelu_p_kernel(tc, x_words, x_scales, w1, w2_words, w2_sca
         pe_table = []
 
         def load_pe(t):
-            pe_table.append(shared.tile([P, T], F32, name=f"pe_table{t}", offset=t * TABLE))
+            pe_table.append(shared.tile([P, T], F32, name=f"pe_table{t}", offset=t * TABLE + (W2_BYTES if t == PACK - 1 else 0)))
             nc.sync.dma_start(out=pe_table[t][:], in_=pe_rows[t])
 
         def load_w1(z):
@@ -72,51 +74,58 @@ def tile_picked_posadd_gelu_p_kernel(tc, x_words, x_scales, w1, w2_words, w2_sca
         load_w1(1)
         load_x(1)
 
-        xs_picked = shared.tile([P, PASSES, S], U8, name="xs_picked", offset=3 * TABLE - S)
+        xs_picked = shared.tile([P, PASSES, S], U8, name="xs_picked", offset=3 * TABLE - 2 * ALIGN)
         for z in range(PASSES):
             nc.vector.tensor_copy(xs_picked[:, z, :], xs_table[:, z, :].indirect(offsets[:]))
-        for q in range(QUADS):
-            first = SPREAD_FROM + SPREAD * ROWS * q
+        for r in range(ROWS):
+            first = SPREAD_FROM + SPREAD * r
             nc.sync.dma_start(
-                out=xs_plane[QUAD * q : QUAD * q + ROWS].rearrange("p z c -> p (z c)").bitcast(I32),
-                in_=xs_picked[first : first + SPREAD * ROWS : SPREAD].rearrange("p z c -> p (z c)").bitcast(I32),
+                out=xs_plane[r:P:QUAD].rearrange("p z c -> p (z c)").bitcast(I32),
+                in_=xs_picked[first : SPREAD_FROM + SPREAD * ROWS * QUADS : SPREAD * ROWS].rearrange("p z c -> p (z c)").bitcast(I32),
             )
         for t in range(PACK):
             load_pe(t)
 
-        acc = [psum.tile([P, S], F32, name=f"acc{t}", tag=f"acc{t}") for t in range(PACK)]
-        for z in range(PASSES):
-            grouped = held.tile([P, PACK, P, PACK], BF16, name=f"w1_grouped{z}", align_bytes=ALIGN)
-            dealt = w1_raw[z][:].rearrange("p j (m t) -> p t m j", t=PACK)
-            nc.vector.tensor_copy(out=grouped[:, : PACK // 2], in_=dealt[:, : PACK // 2])
-            nc.scalar.copy(out=grouped[:, PACK // 2 :], in_=dealt[:, PACK // 2 :])
-            w1_codes = held.tile([P, H], U32, name=f"w1_codes{z}", tag=f"w1_codes{z}", align_bytes=ALIGN)
-            w1_bytes = held.tile([P, H], U8, name=f"w1_bytes{z}", tag=f"w1_bytes{z}", align_bytes=ALIGN)
-            nc.vector.quantize_mx(
-                out=w1_codes[:].bitcast(FP8X4), scales=w1_bytes[:], in_=grouped[:].rearrange("p t m j -> p (t m j)")
-            )
-            x_picked = held.tile([P, S], U32, name=f"x_picked{z}", align_bytes=ALIGN)
-            nc.vector.tensor_copy(x_picked[:], x_table[z][:].bitcast(U32).indirect(offsets[:]))
-            for t in range(PACK):
-                group = slice(t * P, (t + 1) * P)
-                nc.tensor.matmul_mx(
-                    out=acc[t][:],
-                    lhsT=w1_codes[:, group].bitcast(FP8X4),
-                    lhsT_scale=w1_bytes[:, group],
-                    rhs=x_picked[:].bitcast(FP8X4),
-                    rhs_scale=xs_plane[:, z, :],
-                    start=(z == 0),
-                    stop=(z == PASSES - 1),
-                )
-
-        w2_codes = held.tile([P, 2 * N], U8, name="w2_codes", tag="w1_codes0", align_bytes=ALIGN)
-        w2_bytes = held.tile([P, N], U8, name="w2_bytes", tag="w1_bytes0", align_bytes=ALIGN)
+        w2_codes = shared.tile([P, 2 * N], U8, name="w2_codes", offset=3 * TABLE, align_bytes=ALIGN)
+        w2_bytes = shared.tile([P, N], U8, name="w2_bytes", offset=3 * TABLE + 2 * N, align_bytes=ALIGN)
         nc.vector.memset(w2_bytes[:].bitcast(I32), 0)
         nc.sync.dma_start(out=w2_codes[:].bitcast(I32), in_=w2_words[0].bitcast(I32))
         for q in range(QUADS):
             nc.sync.dma_start(
                 out=w2_bytes[QUAD * q : QUAD * q + ROWS, :].bitcast(I32),
                 in_=w2_scales[0, ROWS * q : ROWS * (q + 1), :].bitcast(I32),
+            )
+
+        acc = [psum.tile([P, S], F32, name=f"acc{t}", tag=f"acc{t}") for t in range(PACK)]
+        operands = []
+        for z in range(PASSES):
+            grouped = held.tile([P, PACK, P, PACK], BF16, name=f"w1_grouped{z}", align_bytes=ALIGN)
+            source = w1_raw[z][:].rearrange("p j (m t) -> p m j t", t=PACK)
+            target = grouped[:].rearrange("p t m j -> p m j t")
+            cut = z * P // 2
+            if cut:
+                nc.vector.tensor_copy(out=target[:, :cut], in_=source[:, :cut])
+            nc.scalar.copy(out=target[:, cut:], in_=source[:, cut:])
+            w1_codes = held.tile([P, H], U32, name=f"w1_codes{z}", align_bytes=ALIGN)
+            w1_bytes = held.tile([P, H], U8, name=f"w1_bytes{z}", align_bytes=ALIGN)
+            nc.vector.quantize_mx(
+                out=w1_codes[:].bitcast(FP8X4), scales=w1_bytes[:], in_=grouped[:].rearrange("p t m j -> p (t m j)")
+            )
+            x_picked = held.tile([P, S], U32, name=f"x_picked{z}", align_bytes=ALIGN)
+            nc.vector.tensor_copy(x_picked[:], x_table[z][:].bitcast(U32).indirect(offsets[:]))
+            operands.append((w1_codes, w1_bytes, x_picked))
+        for u, z, e in itertools.product(range(PACK // PAIR), range(PASSES), range(PAIR)):
+            t = PAIR * u + e
+            group = slice(t * P, (t + 1) * P)
+            w1_codes, w1_bytes, x_picked = operands[z]
+            nc.tensor.matmul_mx(
+                out=acc[t][:],
+                lhsT=w1_codes[:, group].bitcast(FP8X4),
+                lhsT_scale=w1_bytes[:, group],
+                rhs=x_picked[:].bitcast(FP8X4),
+                rhs_scale=xs_plane[:, z, :],
+                start=(z == 0),
+                stop=(z == PASSES - 1),
             )
 
         sums = [held.tile([P, S], F32, name=f"sums{t}") for t in range(PACK)]

@@ -153,7 +153,7 @@ def tile_picked_posadd_gelu_p_kernel(tc, x_words, x_scales, w1, w2_words, w2_sca
             gelu(0, c * CHUNK, (c + 1) * CHUNK)
         add_pe(PACK - 2, 0, S)
 
-        cuts = [0, CHUNK // 2] + [c * CHUNK for c in range(1, CHUNKS + 1)]
+        cuts = [c * CHUNK for c in range(CHUNKS + 1)]
         for first, last in zip(cuts[:-1], cuts[1:]):
             add_pe(PACK - 1, first, last)
             gelu(1, first, last)
@@ -177,23 +177,23 @@ def tile_picked_posadd_gelu_p_kernel(tc, x_words, x_scales, w1, w2_words, w2_sca
                 stop=True,
             )
 
+        staged_end = held.tile([P, M_TILES, 2 * CHUNK], F32, name="staged_end")
         for c in range(CHUNKS - 1):
             h_codes, h_bytes = quantize_hidden(c)
             res = psum.tile([P, M_TILES, CHUNK], F32, name=f"res{c}")
             for m in range(M_TILES):
                 second_product(res[:, m, :], m, h_codes, h_bytes)
-            staged = held.tile([P, M_TILES, CHUNK], F32, name=f"staged{c}")
             if c == CHUNKS - 2:
-                nc.vector.tensor_copy(out=staged[:], in_=res[:])
+                nc.scalar.copy(out=staged_end[:, :, :CHUNK], in_=res[:])
             else:
+                staged = held.tile([P, M_TILES, CHUNK], F32, name=f"staged{c}")
                 nc.scalar.copy(out=staged[:], in_=res[:])
-            nc.sync.dma_start(out=out_rows[:, :, c * CHUNK : (c + 1) * CHUNK], in_=staged[:])
+                nc.sync.dma_start(out=out_rows[:, :, c * CHUNK : (c + 1) * CHUNK], in_=staged[:])
 
         h_codes, h_bytes = quantize_hidden(CHUNKS - 1)
         ways_out = (("last", nc.scalar.copy, nc.scalar), ("acc0", nc.vector.tensor_copy, nc.sync))
         for m, (bank, copy_out, queue) in enumerate(ways_out):
             res = psum.tile([P, CHUNK], F32, name=f"last{m}", tag=bank)
             second_product(res[:], m, h_codes, h_bytes)
-            staged = held.tile([P, CHUNK], F32, name=f"staged_last{m}")
-            copy_out(out=staged[:], in_=res[:])
-            queue.dma_start(out=out_rows[:, m, S - CHUNK : S], in_=staged[:])
+            copy_out(out=staged_end[:, m, CHUNK:], in_=res[:])
+            queue.dma_start(out=out_rows[:, m, S - 2 * CHUNK : S], in_=staged_end[:, m, :])

@@ -44,7 +44,7 @@ def tile_picked_posadd_gelu_p_kernel(tc, x_words, x_scales, w1, w2_words, w2_sca
 
         offsets = held.tile([P, S // LIST_COL], U16, name="offsets")
         w1_raw = [held.tile([P, PACK, H], F32, name=f"w1_raw{z}") for z in range(PASSES)]
-        x_table = [held.tile([P, T], I32, name=f"x_table{z}", align_bytes=ALIGN) for z in range(PASSES)]
+        x_table = held.tile([P, PASSES, T], I32, name="x_table", align_bytes=ALIGN)
         xs_table = shared.tile([P, PASSES, T], U8, name="xs_table", offset=TABLE - T)
         xs_plane = held.tile([P, PASSES, S], U8, name="xs_plane", align_bytes=ALIGN)
 
@@ -61,18 +61,14 @@ def tile_picked_posadd_gelu_p_kernel(tc, x_words, x_scales, w1, w2_words, w2_sca
             rows = w1[K_PASS * z : K_PASS * (z + 1), :]
             nc.sync.dma_start(out=w1_raw[z][:], in_=rows.rearrange("(p j) c -> p j c", j=PACK))
 
-        def load_x(z):
-            nc.sync.dma_start(out=x_table[z][:], in_=x_words[z].rearrange("p c r -> p (c r)").bitcast(I32))
-
         load_w1(0)
         nc.sync.dma_start(
             out=xs_table[SPREAD_FROM : SPREAD_FROM + SPREAD * QUADS * ROWS : SPREAD].bitcast(I32),
             in_=x_scales.rearrange("z r c -> r z c").bitcast(I32),
         )
         nc.sync.dma_start(offsets[:], offs)
-        load_x(0)
+        nc.sync.dma_start(out=x_table[:], in_=x_words.rearrange("z p c r -> p z (c r)").bitcast(I32))
         load_w1(1)
-        load_x(1)
 
         xs_picked = shared.tile([P, PASSES, S], U8, name="xs_picked", offset=3 * TABLE - 2 * ALIGN)
         for z in range(PASSES):
@@ -102,7 +98,7 @@ def tile_picked_posadd_gelu_p_kernel(tc, x_words, x_scales, w1, w2_words, w2_sca
             grouped = held.tile([P, PACK, P, PACK], BF16, name=f"w1_grouped{z}", align_bytes=ALIGN)
             source = w1_raw[z][:].rearrange("p j (m t) -> p m j t", t=PACK)
             target = grouped[:].rearrange("p t m j -> p m j t")
-            cut = z * P // 2
+            cut = z * 5 * P // 8
             if cut:
                 nc.vector.tensor_copy(out=target[:, :cut], in_=source[:, :cut])
             nc.scalar.copy(out=target[:, cut:], in_=source[:, cut:])
@@ -112,7 +108,7 @@ def tile_picked_posadd_gelu_p_kernel(tc, x_words, x_scales, w1, w2_words, w2_sca
                 out=w1_codes[:].bitcast(FP8X4), scales=w1_bytes[:], in_=grouped[:].rearrange("p t m j -> p (t m j)")
             )
             x_picked = held.tile([P, S], U32, name=f"x_picked{z}", align_bytes=ALIGN)
-            nc.vector.tensor_copy(x_picked[:], x_table[z][:].bitcast(U32).indirect(offsets[:]))
+            nc.vector.tensor_copy(x_picked[:], x_table[:, z, :].bitcast(U32).indirect(offsets[:]))
             operands.append((w1_codes, w1_bytes, x_picked))
         for u, z, e in itertools.product(range(PACK // PAIR), range(PASSES), range(PAIR)):
             t = PAIR * u + e
@@ -177,23 +173,20 @@ def tile_picked_posadd_gelu_p_kernel(tc, x_words, x_scales, w1, w2_words, w2_sca
                 stop=True,
             )
 
-        staged_end = held.tile([P, M_TILES, 2 * CHUNK], F32, name="staged_end")
         for c in range(CHUNKS - 1):
             h_codes, h_bytes = quantize_hidden(c)
             res = psum.tile([P, M_TILES, CHUNK], F32, name=f"res{c}")
             for m in range(M_TILES):
                 second_product(res[:, m, :], m, h_codes, h_bytes)
-            if c == CHUNKS - 2:
-                nc.scalar.copy(out=staged_end[:, :, :CHUNK], in_=res[:])
-            else:
-                staged = held.tile([P, M_TILES, CHUNK], F32, name=f"staged{c}")
-                nc.scalar.copy(out=staged[:], in_=res[:])
-                nc.sync.dma_start(out=out_rows[:, :, c * CHUNK : (c + 1) * CHUNK], in_=staged[:])
+            staged = held.tile([P, M_TILES, CHUNK], F32, name=f"staged{c}")
+            nc.scalar.copy(out=staged[:], in_=res[:])
+            nc.sync.dma_start(out=out_rows[:, :, c * CHUNK : (c + 1) * CHUNK], in_=staged[:])
 
         h_codes, h_bytes = quantize_hidden(CHUNKS - 1)
-        ways_out = (("last", nc.scalar.copy, nc.scalar), ("acc0", nc.vector.tensor_copy, nc.sync))
-        for m, (bank, copy_out, queue) in enumerate(ways_out):
+        staged = held.tile([P, M_TILES, CHUNK], F32, name="staged_last")
+        ways_out = (("last", nc.scalar.copy), ("acc0", nc.vector.tensor_copy))
+        for m, (bank, copy_out) in enumerate(ways_out):
             res = psum.tile([P, CHUNK], F32, name=f"last{m}", tag=bank)
             second_product(res[:], m, h_codes, h_bytes)
-            copy_out(out=staged_end[:, m, CHUNK:], in_=res[:])
-            queue.dma_start(out=out_rows[:, m, S - 2 * CHUNK : S], in_=staged_end[:, m, :])
+            copy_out(out=staged[:, m, :], in_=res[:])
+        nc.sync.dma_start(out=out_rows[:, :, S - CHUNK : S], in_=staged[:])

@@ -29,9 +29,11 @@ PAIR = 2
 CHUNK = 128
 CHUNKS = S // CHUNK
 M_TILES = N // P
-SPREAD_FROM, SPREAD = 32, 4
+SPREAD_FROM, SPREAD = 32, 2
 TABLE = 4 * T
 W2_BYTES = 3 * N
+GROUPED = 2 * PACK * H
+W2_AT = 3 * TABLE + GROUPED
 ALIGN = 64
 
 
@@ -43,47 +45,44 @@ def tile_picked_posadd_gelu_p_kernel(tc, x_words, x_scales, w1, w2_words, w2_sca
         psum = ctx.enter_context(tc.psum_pool(name="psum", bufs=1))
 
         offsets = held.tile([P, S // LIST_COL], U16, name="offsets")
-        w1_raw = [held.tile([P, PACK, H], F32, name=f"w1_raw{z}") for z in range(PASSES)]
+        w1_raw = held.tile([P, PASSES, PACK, H], F32, name="w1_raw")
         x_table = held.tile([P, PASSES, T], I32, name="x_table", align_bytes=ALIGN)
-        xs_table = shared.tile([P, PASSES, T], U8, name="xs_table", offset=TABLE - T)
-        xs_plane = held.tile([P, PASSES, S], U8, name="xs_plane", align_bytes=ALIGN)
+        xs_table = shared.tile([P, T], U8, name="xs_table", offset=2 * TABLE - T // 2)
+        xs_plane = held.tile([P, S], U8, name="xs_plane", align_bytes=ALIGN)
 
-        nc.vector.memset(xs_table[:].rearrange("p z c -> p (z c)").bitcast(I32), 0)
-        nc.vector.memset(xs_plane[:].rearrange("p z c -> p (z c)").bitcast(I32), 0)
+        nc.vector.memset(xs_table[:].bitcast(I32), 0)
         pe_rows = pe.rearrange("(p t) c -> t p c", t=PACK)
-        pe_table = []
+        pe_table = {}
 
         def load_pe(t):
-            pe_table.append(shared.tile([P, T], F32, name=f"pe_table{t}", offset=t * TABLE + (W2_BYTES if t == PACK - 1 else 0)))
+            pe_table[t] = shared.tile([P, T], F32, name=f"pe_table{t}", offset=t * TABLE + GROUPED + (W2_BYTES if t == PACK - 1 else 0))
             nc.sync.dma_start(out=pe_table[t][:], in_=pe_rows[t])
 
-        def load_w1(z):
-            rows = w1[K_PASS * z : K_PASS * (z + 1), :]
-            nc.sync.dma_start(out=w1_raw[z][:], in_=rows.rearrange("(p j) c -> p j c", j=PACK))
-
-        load_w1(0)
         nc.sync.dma_start(
-            out=xs_table[SPREAD_FROM : SPREAD_FROM + SPREAD * QUADS * ROWS : SPREAD].bitcast(I32),
+            out=w1_raw[:].rearrange("p z j c -> p z (j c)"), in_=w1.rearrange("(z p j) c -> p z (j c)", z=PASSES, j=PACK)
+        )
+        nc.sync.dma_start(
+            out=xs_table[SPREAD_FROM : SPREAD_FROM + SPREAD * PASSES * QUADS * ROWS : SPREAD].bitcast(I32),
             in_=x_scales.rearrange("z r c -> r z c").bitcast(I32),
         )
         nc.sync.dma_start(offsets[:], offs)
         nc.sync.dma_start(out=x_table[:], in_=x_words.rearrange("z p c r -> p z (c r)").bitcast(I32))
-        load_w1(1)
 
-        xs_picked = shared.tile([P, PASSES, S], U8, name="xs_picked", offset=3 * TABLE - 2 * ALIGN)
-        for z in range(PASSES):
-            nc.vector.tensor_copy(xs_picked[:, z, :], xs_table[:, z, :].indirect(offsets[:]))
+        xs_picked = shared.tile([P, W2_BYTES + 2 * ALIGN], U8, name="xs_picked", offset=W2_AT - ALIGN)
+        nc.vector.tensor_copy(xs_picked[:, :S], xs_table[:].indirect(offsets[:]))
         for r in range(ROWS):
-            first = SPREAD_FROM + SPREAD * r
+            first = SPREAD_FROM + SPREAD * PASSES * r
             nc.sync.dma_start(
-                out=xs_plane[r:P:QUAD].rearrange("p z c -> p (z c)").bitcast(I32),
-                in_=xs_picked[first : SPREAD_FROM + SPREAD * ROWS * QUADS : SPREAD * ROWS].rearrange("p z c -> p (z c)").bitcast(I32),
+                out=xs_plane[r:P:ROWS].bitcast(I32),
+                in_=xs_picked[first : first + SPREAD * (P // ROWS) : SPREAD, :S].bitcast(I32),
             )
-        for t in range(PACK):
+        pe_table[0] = shared.tile([P, PAIR * T], F32, name="pe_table01", offset=0)
+        nc.sync.dma_start(out=pe_table[0][:], in_=pe.rearrange("(p u e) c -> u p (e c)", u=PACK // PAIR, e=PAIR)[0])
+        for t in range(PAIR, PACK):
             load_pe(t)
 
-        w2_codes = shared.tile([P, 2 * N], U8, name="w2_codes", offset=3 * TABLE, align_bytes=ALIGN)
-        w2_bytes = shared.tile([P, N], U8, name="w2_bytes", offset=3 * TABLE + 2 * N, align_bytes=ALIGN)
+        w2_codes = shared.tile([P, 2 * N], U8, name="w2_codes", offset=W2_AT, align_bytes=ALIGN)
+        w2_bytes = shared.tile([P, N], U8, name="w2_bytes", offset=W2_AT + 2 * N, align_bytes=ALIGN)
         nc.vector.memset(w2_bytes[:].bitcast(I32), 0)
         nc.sync.dma_start(out=w2_codes[:].bitcast(I32), in_=w2_words[0].bitcast(I32))
         for q in range(QUADS):
@@ -95,13 +94,13 @@ def tile_picked_posadd_gelu_p_kernel(tc, x_words, x_scales, w1, w2_words, w2_sca
         acc = [psum.tile([P, S], F32, name=f"acc{t}", tag=f"acc{t}") for t in range(PACK)]
         operands = []
         for z in range(PASSES):
-            grouped = held.tile([P, PACK, P, PACK], BF16, name=f"w1_grouped{z}", align_bytes=ALIGN)
-            source = w1_raw[z][:].rearrange("p j (m t) -> p m j t", t=PACK)
+            if z:
+                grouped = shared.tile([P, PACK, P, PACK], BF16, name="w1_grouped1", offset=2 * TABLE, align_bytes=ALIGN)
+            else:
+                grouped = held.tile([P, PACK, P, PACK], BF16, name="w1_grouped0", align_bytes=ALIGN)
+            source = w1_raw[:, z].rearrange("p j (m t) -> p m j t", t=PACK)
             target = grouped[:].rearrange("p t m j -> p m j t")
-            cut = z * 5 * P // 8
-            if cut:
-                nc.vector.tensor_copy(out=target[:, :cut], in_=source[:, :cut])
-            nc.scalar.copy(out=target[:, cut:], in_=source[:, cut:])
+            (nc.vector.tensor_copy if z else nc.scalar.copy)(out=target, in_=source)
             w1_codes = held.tile([P, H], U32, name=f"w1_codes{z}", align_bytes=ALIGN)
             w1_bytes = held.tile([P, H], U8, name=f"w1_bytes{z}", align_bytes=ALIGN)
             nc.vector.quantize_mx(
@@ -110,7 +109,7 @@ def tile_picked_posadd_gelu_p_kernel(tc, x_words, x_scales, w1, w2_words, w2_sca
             x_picked = held.tile([P, S], U32, name=f"x_picked{z}", align_bytes=ALIGN)
             nc.vector.tensor_copy(x_picked[:], x_table[:, z, :].bitcast(U32).indirect(offsets[:]))
             operands.append((w1_codes, w1_bytes, x_picked))
-        for u, z, e in itertools.product(range(PACK // PAIR), range(PASSES), range(PAIR)):
+        for u, z, e in itertools.product(reversed(range(PACK // PAIR)), range(PASSES), range(PAIR)):
             t = PAIR * u + e
             group = slice(t * P, (t + 1) * P)
             w1_codes, w1_bytes, x_picked = operands[z]
@@ -119,13 +118,13 @@ def tile_picked_posadd_gelu_p_kernel(tc, x_words, x_scales, w1, w2_words, w2_sca
                 lhsT=w1_codes[:, group].bitcast(FP8X4),
                 lhsT_scale=w1_bytes[:, group],
                 rhs=x_picked[:].bitcast(FP8X4),
-                rhs_scale=xs_plane[:, z, :],
+                rhs_scale=xs_plane[ROWS * z : P, :],
                 start=(z == 0),
                 stop=(z == PASSES - 1),
             )
 
-        sums = [held.tile([P, S], F32, name=f"sums{t}") for t in range(PACK)]
-        for t in range(PACK):
+        sums = {t: held.tile([P, S], F32, name=f"sums{t}") for t in (2, 3, 0)}
+        for t in (2, 3, 0):
             nc.scalar.copy(out=sums[t][:], in_=acc[t][:])
 
         pre = [held.tile([P, PAIR, S], F32, name=f"pre{u}") for u in range(PACK // PAIR)]
@@ -143,8 +142,11 @@ def tile_picked_posadd_gelu_p_kernel(tc, x_words, x_scales, w1, w2_words, w2_sca
                 GELU,
             )
 
-        for t in range(PAIR):
-            add_pe(t, 0, S)
+        pe_picked = held.tile([P, S], F32, name="pe_picked")
+        nc.vector.tensor_copy(pe_picked[:], pe_table[0][:, T:].indirect(offsets[:]))
+        nc.vector.tensor_tensor(pre[0][:, 1, :], acc[1][:], pe_picked[:], ADD)
+        add_pe(0, 0, S // 2)
+        add_pe(0, S // 2, S)
         for c in range(CHUNKS):
             gelu(0, c * CHUNK, (c + 1) * CHUNK)
         add_pe(PACK - 2, 0, S)

@@ -15,6 +15,7 @@ U8 = mybir.dt.uint8
 FP8X4 = mybir.dt.float8_e4m3fn_x4
 FP4X4 = mybir.dt.float4_e2m1fn_x4
 GELU = mybir.ActivationFunctionType.Gelu_apprx_tanh
+COPY = mybir.ActivationFunctionType.Copy
 ADD = mybir.AluOpType.add
 
 P = 128
@@ -51,6 +52,9 @@ def tile_picked_posadd_gelu_p_kernel(tc, x_words, x_scales, w1, w2_words, w2_sca
         xs_plane = held.tile([P, S], U8, name="xs_plane", align_bytes=ALIGN)
 
         nc.vector.memset(xs_table[:].bitcast(I32), 0)
+        warm = held.tile([P, 2, 8], F32, name="warm")
+        nc.vector.memset(warm[:, 0, :], 0.0)
+        nc.scalar.activation(warm[:, 1, :], warm[:, 0, :], GELU)
         pe_rows = pe.rearrange("(p t) c -> t p c", t=PACK)
         pe_table = {}
 
@@ -109,8 +113,8 @@ def tile_picked_posadd_gelu_p_kernel(tc, x_words, x_scales, w1, w2_words, w2_sca
             x_picked = held.tile([P, S], U32, name=f"x_picked{z}", align_bytes=ALIGN)
             nc.vector.tensor_copy(x_picked[:], x_table[:, z, :].bitcast(U32).indirect(offsets[:]))
             operands.append((w1_codes, w1_bytes, x_picked))
-        for u, z, e in itertools.product(reversed(range(PACK // PAIR)), range(PASSES), range(PAIR)):
-            t = PAIR * u + e
+        for groups, z, e in itertools.product(((0, 3), (2, 1)), range(PASSES), range(PAIR)):
+            t = groups[e]
             group = slice(t * P, (t + 1) * P)
             w1_codes, w1_bytes, x_picked = operands[z]
             nc.tensor.matmul_mx(
@@ -123,37 +127,45 @@ def tile_picked_posadd_gelu_p_kernel(tc, x_words, x_scales, w1, w2_words, w2_sca
                 stop=(z == PASSES - 1),
             )
 
-        sums = {t: held.tile([P, S], F32, name=f"sums{t}") for t in (2, 3, 0)}
-        for t in (2, 3, 0):
-            nc.scalar.copy(out=sums[t][:], in_=acc[t][:])
+        sums = {t: held.tile([P, S], F32, name=f"sums{t}") for t in (0, 3)}
+        nc.scalar.copy(out=sums[0][:], in_=acc[0][:])
+        nc.vector.tensor_copy(out=sums[3][:], in_=acc[3][:])
+        pe_picked = held.tile([P, S], F32, name="pe_picked")
+        nc.scalar.activation(pe_picked[:], pe_table[0][:, T:].indirect(offsets[:]), COPY)
 
         pre = [held.tile([P, PAIR, S], F32, name=f"pre{u}") for u in range(PACK // PAIR)]
-        hidden = [held.tile([P, CHUNK, PACK], BF16, name=f"hidden{c}", align_bytes=ALIGN) for c in range(CHUNKS)]
+        hidden = held.tile([P, S, PACK], BF16, name="hidden", align_bytes=ALIGN)
 
         def add_pe(t, first, last):
             entries = offsets[:, first // LIST_COL : last // LIST_COL]
             nc.vector.tensor_tensor(pre[t // PAIR][:, t % PAIR, first:last], pe_table[t][:].indirect(entries), sums[t][:, first:last], ADD)
 
         def gelu(u, first, last):
-            c, n = divmod(first, CHUNK)
             nc.scalar.activation(
-                hidden[c][:, n : n + last - first, PAIR * u : PAIR * (u + 1)],
+                hidden[:, first:last, PAIR * u : PAIR * (u + 1)],
                 pre[u][:, :, first:last].rearrange("p e j -> p j e"),
                 GELU,
             )
 
-        pe_picked = held.tile([P, S], F32, name="pe_picked")
-        nc.vector.tensor_copy(pe_picked[:], pe_table[0][:, T:].indirect(offsets[:]))
+        add_pe(0, 0, S)
+        sums[2] = shared.tile([P, S], F32, name="sums2", offset=0)
+        nc.scalar.copy(out=sums[2][:], in_=acc[2][:])
         nc.vector.tensor_tensor(pre[0][:, 1, :], acc[1][:], pe_picked[:], ADD)
-        add_pe(0, 0, S // 2)
-        add_pe(0, S // 2, S)
         for c in range(CHUNKS):
             gelu(0, c * CHUNK, (c + 1) * CHUNK)
         add_pe(PACK - 2, 0, S)
 
-        cuts = [c * CHUNK for c in range(CHUNKS + 1)]
+        half = CHUNK // 2
+        fetched_from = S - CHUNK
+        cuts = list(range(0, fetched_from + 1, half)) + [S]
+        fetched = held.tile([P, CHUNK], F32, name="fetched")
+        entries = offsets[:, fetched_from // LIST_COL : (fetched_from + CHUNK) // LIST_COL]
+        nc.scalar.activation(fetched[:], pe_table[PACK - 1][:].indirect(entries), COPY)
         for first, last in zip(cuts[:-1], cuts[1:]):
-            add_pe(PACK - 1, first, last)
+            if first == fetched_from:
+                nc.vector.tensor_tensor(pre[1][:, 1, first:last], fetched[:], sums[PACK - 1][:, first:last], ADD)
+            else:
+                add_pe(PACK - 1, first, last)
             gelu(1, first, last)
 
         out_rows = out.rearrange("(m p) j -> p m j", p=P)
@@ -161,7 +173,7 @@ def tile_picked_posadd_gelu_p_kernel(tc, x_words, x_scales, w1, w2_words, w2_sca
         def quantize_hidden(c):
             h_codes = held.tile([P, CHUNK], U32, name=f"h_codes{c}", align_bytes=ALIGN)
             h_bytes = held.tile([P, CHUNK], U8, name=f"h_bytes{c}", align_bytes=ALIGN)
-            nc.vector.quantize_mx(out=h_codes[:].bitcast(FP8X4), scales=h_bytes[:], in_=hidden[c][:].rearrange("p n t -> p (n t)"))
+            nc.vector.quantize_mx(out=h_codes[:].bitcast(FP8X4), scales=h_bytes[:], in_=hidden[:, c * CHUNK : (c + 1) * CHUNK, :].rearrange("p n t -> p (n t)"))
             return h_codes, h_bytes
 
         def second_product(result, m, h_codes, h_bytes):

@@ -166,14 +166,21 @@ def tile_picked_posadd_gelu_p_kernel(tc, x_words, x_scales, w1, w2_words, w2_sca
                 nc.vector.tensor_tensor(pre[1][:, 1, first:last], fetched[:], sums[PACK - 1][:, first:last], ADD)
             else:
                 add_pe(PACK - 1, first, last)
-            gelu(1, first, last)
+            for piece in range(first, last, half):
+                gelu(1, piece, piece + half)
 
         out_rows = out.rearrange("(m p) j -> p m j", p=P)
 
         def quantize_hidden(c):
             h_codes = held.tile([P, CHUNK], U32, name=f"h_codes{c}", align_bytes=ALIGN)
             h_bytes = held.tile([P, CHUNK], U8, name=f"h_bytes{c}", align_bytes=ALIGN)
-            nc.vector.quantize_mx(out=h_codes[:].bitcast(FP8X4), scales=h_bytes[:], in_=hidden[:, c * CHUNK : (c + 1) * CHUNK, :].rearrange("p n t -> p (n t)"))
+            width = half if c == CHUNKS - 1 else CHUNK
+            for n in range(0, CHUNK, width):
+                nc.vector.quantize_mx(
+                    out=h_codes[:, n : n + width].bitcast(FP8X4),
+                    scales=h_bytes[:, n : n + width],
+                    in_=hidden[:, c * CHUNK + n : c * CHUNK + n + width, :].rearrange("p n t -> p (n t)"),
+                )
             return h_codes, h_bytes
 
         def second_product(result, m, h_codes, h_bytes):
@@ -187,20 +194,15 @@ def tile_picked_posadd_gelu_p_kernel(tc, x_words, x_scales, w1, w2_words, w2_sca
                 stop=True,
             )
 
-        for c in range(CHUNKS - 1):
+        for c in range(CHUNKS):
             h_codes, h_bytes = quantize_hidden(c)
-            res = psum.tile([P, M_TILES, CHUNK], F32, name=f"res{c}")
-            for m in range(M_TILES):
-                second_product(res[:, m, :], m, h_codes, h_bytes)
             staged = held.tile([P, M_TILES, CHUNK], F32, name=f"staged{c}")
-            nc.scalar.copy(out=staged[:], in_=res[:])
-            nc.sync.dma_start(out=out_rows[:, :, c * CHUNK : (c + 1) * CHUNK], in_=staged[:])
-
-        h_codes, h_bytes = quantize_hidden(CHUNKS - 1)
-        staged = held.tile([P, M_TILES, CHUNK], F32, name="staged_last")
-        ways_out = (("last", nc.scalar.copy), ("acc0", nc.vector.tensor_copy))
-        for m, (bank, copy_out) in enumerate(ways_out):
-            res = psum.tile([P, CHUNK], F32, name=f"last{m}", tag=bank)
-            second_product(res[:], m, h_codes, h_bytes)
-            copy_out(out=staged[:, m, :], in_=res[:])
-        nc.sync.dma_start(out=out_rows[:, :, S - CHUNK : S], in_=staged[:])
+            ways_out = ((f"res{c}", nc.scalar.copy), (f"acc{c}", nc.vector.tensor_copy if c else nc.scalar.copy))
+            for m, (bank, copy_out) in enumerate(ways_out):
+                res = psum.tile([P, CHUNK], F32, name=f"res{c}_{m}", tag=bank)
+                second_product(res[:], m, h_codes, h_bytes)
+                copy_out(out=staged[:, m, :], in_=res[:])
+                if c in (0, CHUNKS - 1):
+                    nc.sync.dma_start(out=out_rows[:, m, c * CHUNK : (c + 1) * CHUNK], in_=staged[:, m, :])
+            if 0 < c < CHUNKS - 1:
+                nc.sync.dma_start(out=out_rows[:, :, c * CHUNK : (c + 1) * CHUNK], in_=staged[:])

@@ -155,26 +155,12 @@ def tile_picked_posadd_gelu_p_kernel(tc, x_words, x_scales, w1, w2_words, w2_sca
             gelu(0, c * CHUNK, (c + 1) * CHUNK)
         add_pe(PACK - 2, 0, S)
 
-        half = CHUNK // 2
-        fetched_from = S - CHUNK
-        cuts = list(range(0, fetched_from + 1, half)) + [S]
-        fetched = held.tile([P, CHUNK], F32, name="fetched")
-        entries = offsets[:, fetched_from // LIST_COL : (fetched_from + CHUNK) // LIST_COL]
-        nc.scalar.activation(fetched[:], pe_table[PACK - 1][:].indirect(entries), COPY)
-        for first, last in zip(cuts[:-1], cuts[1:]):
-            if first == fetched_from:
-                nc.vector.tensor_tensor(pre[1][:, 1, first:last], fetched[:], sums[PACK - 1][:, first:last], ADD)
-            else:
-                add_pe(PACK - 1, first, last)
-            for piece in range(first, last, half):
-                gelu(1, piece, piece + half)
-
         out_rows = out.rearrange("(m p) j -> p m j", p=P)
 
         def quantize_hidden(c):
             h_codes = held.tile([P, CHUNK], U32, name=f"h_codes{c}", align_bytes=ALIGN)
             h_bytes = held.tile([P, CHUNK], U8, name=f"h_bytes{c}", align_bytes=ALIGN)
-            width = half if c == CHUNKS - 1 else CHUNK
+            width = CHUNK // 2 if c == CHUNKS - 1 else CHUNK
             for n in range(0, CHUNK, width):
                 nc.vector.quantize_mx(
                     out=h_codes[:, n : n + width].bitcast(FP8X4),
@@ -194,15 +180,38 @@ def tile_picked_posadd_gelu_p_kernel(tc, x_words, x_scales, w1, w2_words, w2_sca
                 stop=True,
             )
 
+        half = CHUNK // 2
+        fetched_from, held_from = S - CHUNK - half, S - half
+        fetched = held.tile([P, CHUNK], F32, name="fetched")
+        entries = offsets[:, fetched_from // LIST_COL : held_from // LIST_COL]
+        nc.scalar.activation(fetched[:], pe_table[PACK - 1][:].indirect(entries), COPY)
+        for first in range(0, fetched_from, half):
+            add_pe(PACK - 1, first, first + half)
+            gelu(1, first, first + half)
+        nc.vector.tensor_tensor(pre[1][:, 1, fetched_from:held_from], fetched[:], sums[PACK - 1][:, fetched_from:held_from], ADD)
+        for first in range(fetched_from, held_from, half):
+            gelu(1, first, first + half)
+        first_codes = quantize_hidden(0)
+        nc.vector.tensor_tensor(
+            pre[1][:, 1, half:CHUNK],
+            pe_table[PACK - 1][:].indirect(offsets[:, held_from // LIST_COL :]),
+            sums[PACK - 1][:, held_from:],
+            ADD,
+        )
+        apart = S + half - held_from
+        last_pair = pre[1][:].rearrange("p e j -> p (e j)")[:, held_from : held_from + 2 * apart].rearrange("p (e j) -> p j e", e=PAIR)
+        nc.scalar.activation(hidden[:, held_from:, PAIR:], last_pair[:, :half, :], GELU)
+
+        staged = [held.tile([P, S], F32, name=f"staged{m}") for m in range(M_TILES)]
         for c in range(CHUNKS):
-            h_codes, h_bytes = quantize_hidden(c)
-            staged = held.tile([P, M_TILES, CHUNK], F32, name=f"staged{c}")
+            h_codes, h_bytes = quantize_hidden(c) if c else first_codes
+            tokens = slice(c * CHUNK, (c + 1) * CHUNK)
             ways_out = ((f"res{c}", nc.scalar.copy), (f"acc{c}", nc.vector.tensor_copy if c else nc.scalar.copy))
             for m, (bank, copy_out) in enumerate(ways_out):
                 res = psum.tile([P, CHUNK], F32, name=f"res{c}_{m}", tag=bank)
                 second_product(res[:], m, h_codes, h_bytes)
-                copy_out(out=staged[:, m, :], in_=res[:])
-                if c in (0, CHUNKS - 1):
-                    nc.sync.dma_start(out=out_rows[:, m, c * CHUNK : (c + 1) * CHUNK], in_=staged[:, m, :])
-            if 0 < c < CHUNKS - 1:
-                nc.sync.dma_start(out=out_rows[:, :, c * CHUNK : (c + 1) * CHUNK], in_=staged[:])
+                copy_out(out=staged[m][:, tokens], in_=res[:])
+                if m and c == CHUNKS - 2:
+                    continue
+                stored = slice((c - 1) * CHUNK, S) if m and c == CHUNKS - 1 else tokens
+                nc.sync.dma_start(out=out_rows[:, m, stored], in_=staged[m][:, stored])

@@ -27,15 +27,23 @@ QUAD = P // QUADS
 ROWS = 4
 LIST_COL = 16
 PAIR = 2
+LAST = PACK - 1
 CHUNK = 128
 CHUNKS = S // CHUNK
+PIECE = CHUNK // 2
 M_TILES = N // P
-SPREAD_FROM, SPREAD = 32, 2
-TABLE = 4 * T
-W2_BYTES = 3 * N
-GROUPED = 2 * PACK * H
-W2_AT = 3 * TABLE + GROUPED
+WARM = 8
 ALIGN = 64
+
+SPREAD_FROM, SPREAD = 32, 2
+
+TABLE = 4 * T
+GROUPED = 2 * PACK * H
+W2_BYTES = 3 * N
+GROUPED_AT = PAIR * TABLE
+XS_TABLE_AT = GROUPED_AT - T // 2
+W2_AT = GROUPED_AT + GROUPED + TABLE
+TABLE_AT = {2: GROUPED_AT + GROUPED, 3: W2_AT + W2_BYTES}
 
 
 def tile_picked_posadd_gelu_p_kernel(tc, x_words, x_scales, w1, w2_words, w2_scales, pe, offs, out):
@@ -48,19 +56,14 @@ def tile_picked_posadd_gelu_p_kernel(tc, x_words, x_scales, w1, w2_words, w2_sca
         offsets = held.tile([P, S // LIST_COL], U16, name="offsets")
         w1_raw = held.tile([P, PASSES, PACK, H], F32, name="w1_raw")
         x_table = held.tile([P, PASSES, T], I32, name="x_table", align_bytes=ALIGN)
-        xs_table = shared.tile([P, T], U8, name="xs_table", offset=2 * TABLE - T // 2)
+        xs_table = shared.tile([P, T], U8, name="xs_table", offset=XS_TABLE_AT)
         xs_plane = held.tile([P, S], U8, name="xs_plane", align_bytes=ALIGN)
 
         nc.vector.memset(xs_table[:].bitcast(I32), 0)
-        warm = held.tile([P, 2, 8], F32, name="warm")
+
+        warm = held.tile([P, 2, WARM], F32, name="warm")
         nc.vector.memset(warm[:, 0, :], 0.0)
         nc.scalar.activation(warm[:, 1, :], warm[:, 0, :], GELU)
-        pe_rows = pe.rearrange("(p t) c -> t p c", t=PACK)
-        pe_table = {}
-
-        def load_pe(t):
-            pe_table[t] = shared.tile([P, T], F32, name=f"pe_table{t}", offset=t * TABLE + GROUPED + (W2_BYTES if t == PACK - 1 else 0))
-            nc.sync.dma_start(out=pe_table[t][:], in_=pe_rows[t])
 
         nc.sync.dma_start(
             out=w1_raw[:].rearrange("p z j c -> p z (j c)"), in_=w1.rearrange("(z p j) c -> p z (j c)", z=PASSES, j=PACK)
@@ -80,10 +83,13 @@ def tile_picked_posadd_gelu_p_kernel(tc, x_words, x_scales, w1, w2_words, w2_sca
                 out=xs_plane[r:P:ROWS].bitcast(I32),
                 in_=xs_picked[first : first + SPREAD * (P // ROWS) : SPREAD, :S].bitcast(I32),
             )
-        pe_table[0] = shared.tile([P, PAIR * T], F32, name="pe_table01", offset=0)
-        nc.sync.dma_start(out=pe_table[0][:], in_=pe.rearrange("(p u e) c -> u p (e c)", u=PACK // PAIR, e=PAIR)[0])
+
+        first_tables = shared.tile([P, PAIR * T], F32, name="pe_table01", offset=0)
+        nc.sync.dma_start(out=first_tables[:], in_=pe.rearrange("(p u e) c -> u p (e c)", u=PACK // PAIR, e=PAIR)[0])
+        pe_table = {0: first_tables}
         for t in range(PAIR, PACK):
-            load_pe(t)
+            pe_table[t] = shared.tile([P, T], F32, name=f"pe_table{t}", offset=TABLE_AT[t])
+            nc.sync.dma_start(out=pe_table[t][:], in_=pe.rearrange("(p t) c -> t p c", t=PACK)[t])
 
         w2_codes = shared.tile([P, 2 * N], U8, name="w2_codes", offset=W2_AT, align_bytes=ALIGN)
         w2_bytes = shared.tile([P, N], U8, name="w2_bytes", offset=W2_AT + 2 * N, align_bytes=ALIGN)
@@ -96,15 +102,14 @@ def tile_picked_posadd_gelu_p_kernel(tc, x_words, x_scales, w1, w2_words, w2_sca
             )
 
         acc = [psum.tile([P, S], F32, name=f"acc{t}", tag=f"acc{t}") for t in range(PACK)]
+        grouped_tiles = (
+            lambda: held.tile([P, PACK, P, PACK], BF16, name="w1_grouped0", align_bytes=ALIGN),
+            lambda: shared.tile([P, PACK, P, PACK], BF16, name="w1_grouped1", offset=GROUPED_AT, align_bytes=ALIGN),
+        )
         operands = []
-        for z in range(PASSES):
-            if z:
-                grouped = shared.tile([P, PACK, P, PACK], BF16, name="w1_grouped1", offset=2 * TABLE, align_bytes=ALIGN)
-            else:
-                grouped = held.tile([P, PACK, P, PACK], BF16, name="w1_grouped0", align_bytes=ALIGN)
-            source = w1_raw[:, z].rearrange("p j (m t) -> p m j t", t=PACK)
-            target = grouped[:].rearrange("p t m j -> p m j t")
-            (nc.vector.tensor_copy if z else nc.scalar.copy)(out=target, in_=source)
+        for z, round_copy in enumerate((nc.scalar.copy, nc.vector.tensor_copy)):
+            grouped = grouped_tiles[z]()
+            round_copy(out=grouped[:].rearrange("p t m j -> p m j t"), in_=w1_raw[:, z].rearrange("p j (m t) -> p m j t", t=PACK))
             w1_codes = held.tile([P, H], U32, name=f"w1_codes{z}", align_bytes=ALIGN)
             w1_bytes = held.tile([P, H], U8, name=f"w1_bytes{z}", align_bytes=ALIGN)
             nc.vector.quantize_mx(
@@ -113,39 +118,51 @@ def tile_picked_posadd_gelu_p_kernel(tc, x_words, x_scales, w1, w2_words, w2_sca
             x_picked = held.tile([P, S], U32, name=f"x_picked{z}", align_bytes=ALIGN)
             nc.vector.tensor_copy(x_picked[:], x_table[:, z, :].bitcast(U32).indirect(offsets[:]))
             operands.append((w1_codes, w1_bytes, x_picked))
-        for groups, z, e in itertools.product(((0, 3), (2, 1)), range(PASSES), range(PAIR)):
+
+        for groups, z, e in itertools.product(((0, LAST), (2, 1)), range(PASSES), range(PAIR)):
             t = groups[e]
-            group = slice(t * P, (t + 1) * P)
+            columns = slice(t * P, (t + 1) * P)
             w1_codes, w1_bytes, x_picked = operands[z]
             nc.tensor.matmul_mx(
                 out=acc[t][:],
-                lhsT=w1_codes[:, group].bitcast(FP8X4),
-                lhsT_scale=w1_bytes[:, group],
+                lhsT=w1_codes[:, columns].bitcast(FP8X4),
+                lhsT_scale=w1_bytes[:, columns],
                 rhs=x_picked[:].bitcast(FP8X4),
                 rhs_scale=xs_plane[ROWS * z : P, :],
                 start=(z == 0),
                 stop=(z == PASSES - 1),
             )
 
-        sums = {t: held.tile([P, S], F32, name=f"sums{t}") for t in (0, 3)}
+        sums = {t: held.tile([P, S], F32, name=f"sums{t}") for t in (0, LAST)}
         nc.scalar.copy(out=sums[0][:], in_=acc[0][:])
-        nc.vector.tensor_copy(out=sums[3][:], in_=acc[3][:])
+        nc.vector.tensor_copy(out=sums[LAST][:], in_=acc[LAST][:])
         pe_picked = held.tile([P, S], F32, name="pe_picked")
-        nc.scalar.activation(pe_picked[:], pe_table[0][:, T:].indirect(offsets[:]), COPY)
+        nc.scalar.activation(pe_picked[:], first_tables[:, T:].indirect(offsets[:]), COPY)
 
         pre = [held.tile([P, PAIR, S], F32, name=f"pre{u}") for u in range(PACK // PAIR)]
         hidden = held.tile([P, S, PACK], BF16, name="hidden", align_bytes=ALIGN)
 
+        def looked_up(t, first, last):
+            return pe_table[t][:].indirect(offsets[:, first // LIST_COL : last // LIST_COL])
+
         def add_pe(t, first, last):
-            entries = offsets[:, first // LIST_COL : last // LIST_COL]
-            nc.vector.tensor_tensor(pre[t // PAIR][:, t % PAIR, first:last], pe_table[t][:].indirect(entries), sums[t][:, first:last], ADD)
+            nc.vector.tensor_tensor(pre[t // PAIR][:, t % PAIR, first:last], looked_up(t, first, last), sums[t][:, first:last], ADD)
 
         def gelu(u, first, last):
             nc.scalar.activation(
-                hidden[:, first:last, PAIR * u : PAIR * (u + 1)],
-                pre[u][:, :, first:last].rearrange("p e j -> p j e"),
-                GELU,
+                hidden[:, first:last, PAIR * u : PAIR * (u + 1)], pre[u][:, :, first:last].rearrange("p e j -> p j e"), GELU
             )
+
+        def quantize_hidden(c, cuts):
+            h_codes = held.tile([P, CHUNK], U32, name=f"h_codes{c}", align_bytes=ALIGN)
+            h_bytes = held.tile([P, CHUNK], U8, name=f"h_bytes{c}", align_bytes=ALIGN)
+            for first, last in zip(cuts[:-1], cuts[1:]):
+                nc.vector.quantize_mx(
+                    out=h_codes[:, first:last].bitcast(FP8X4),
+                    scales=h_bytes[:, first:last],
+                    in_=hidden[:, c * CHUNK + first : c * CHUNK + last, :].rearrange("p n t -> p (n t)"),
+                )
+            return h_codes, h_bytes
 
         add_pe(0, 0, S)
         sums[2] = shared.tile([P, S], F32, name="sums2", offset=0)
@@ -153,65 +170,51 @@ def tile_picked_posadd_gelu_p_kernel(tc, x_words, x_scales, w1, w2_words, w2_sca
         nc.vector.tensor_tensor(pre[0][:, 1, :], acc[1][:], pe_picked[:], ADD)
         for c in range(CHUNKS):
             gelu(0, c * CHUNK, (c + 1) * CHUNK)
-        add_pe(PACK - 2, 0, S)
+        add_pe(2, 0, S)
+
+        final_from = S - PIECE
+        fetched_from = final_from - 2 * PIECE
+        fetched = held.tile([P, final_from - fetched_from], F32, name="fetched")
+        nc.scalar.activation(fetched[:], looked_up(LAST, fetched_from, final_from), COPY)
+        for first in range(0, fetched_from, PIECE):
+            add_pe(LAST, first, first + PIECE)
+            gelu(1, first, first + PIECE)
+        nc.vector.tensor_tensor(pre[1][:, 1, fetched_from:final_from], fetched[:], sums[LAST][:, fetched_from:final_from], ADD)
+        for first in range(fetched_from, final_from, PIECE):
+            gelu(1, first, first + PIECE)
+
+        whole = (0, CHUNK)
+        quantized = {0: quantize_hidden(0, whole)}
+        nc.vector.tensor_tensor(pre[1][:, 1, PIECE:CHUNK], looked_up(LAST, final_from, S), sums[LAST][:, final_from:], ADD)
+        apart = S + PIECE - final_from
+        final_pair = pre[1][:].rearrange("p e j -> p (e j)")[:, final_from : final_from + PAIR * apart].rearrange("p (e j) -> p j e", e=PAIR)
+        last_cuts = (0, PIECE, PIECE + PIECE // 2, CHUNK)
+        for first in range(0, PIECE, PIECE // 2):
+            last = first + PIECE // 2
+            nc.scalar.activation(hidden[:, final_from + first : final_from + last, PAIR:], final_pair[:, first:last, :], GELU)
 
         out_rows = out.rearrange("(m p) j -> p m j", p=P)
-
-        def quantize_hidden(c):
-            h_codes = held.tile([P, CHUNK], U32, name=f"h_codes{c}", align_bytes=ALIGN)
-            h_bytes = held.tile([P, CHUNK], U8, name=f"h_bytes{c}", align_bytes=ALIGN)
-            width = CHUNK // 2 if c == CHUNKS - 1 else CHUNK
-            for n in range(0, CHUNK, width):
-                nc.vector.quantize_mx(
-                    out=h_codes[:, n : n + width].bitcast(FP8X4),
-                    scales=h_bytes[:, n : n + width],
-                    in_=hidden[:, c * CHUNK + n : c * CHUNK + n + width, :].rearrange("p n t -> p (n t)"),
-                )
-            return h_codes, h_bytes
-
-        def second_product(result, m, h_codes, h_bytes):
-            nc.tensor.matmul_mx(
-                out=result,
-                lhsT=w2_codes[:, 2 * m * P : 2 * (m + 1) * P].bitcast(FP4X4),
-                lhsT_scale=w2_bytes[:, m * P : (m + 1) * P],
-                rhs=h_codes[:].bitcast(FP8X4),
-                rhs_scale=h_bytes[:],
-                start=True,
-                stop=True,
-            )
-
-        half = CHUNK // 2
-        fetched_from, held_from = S - CHUNK - half, S - half
-        fetched = held.tile([P, CHUNK], F32, name="fetched")
-        entries = offsets[:, fetched_from // LIST_COL : held_from // LIST_COL]
-        nc.scalar.activation(fetched[:], pe_table[PACK - 1][:].indirect(entries), COPY)
-        for first in range(0, fetched_from, half):
-            add_pe(PACK - 1, first, first + half)
-            gelu(1, first, first + half)
-        nc.vector.tensor_tensor(pre[1][:, 1, fetched_from:held_from], fetched[:], sums[PACK - 1][:, fetched_from:held_from], ADD)
-        for first in range(fetched_from, held_from, half):
-            gelu(1, first, first + half)
-        first_codes = quantize_hidden(0)
-        nc.vector.tensor_tensor(
-            pre[1][:, 1, half:CHUNK],
-            pe_table[PACK - 1][:].indirect(offsets[:, held_from // LIST_COL :]),
-            sums[PACK - 1][:, held_from:],
-            ADD,
-        )
-        apart = S + half - held_from
-        last_pair = pre[1][:].rearrange("p e j -> p (e j)")[:, held_from : held_from + 2 * apart].rearrange("p (e j) -> p j e", e=PAIR)
-        nc.scalar.activation(hidden[:, held_from:, PAIR:], last_pair[:, :half, :], GELU)
-
         staged = [held.tile([P, S], F32, name=f"staged{m}") for m in range(M_TILES)]
         for c in range(CHUNKS):
-            h_codes, h_bytes = quantize_hidden(c) if c else first_codes
+            if c not in quantized:
+                quantized[c] = quantize_hidden(c, last_cuts if c == CHUNKS - 1 else whole)
+            h_codes, h_bytes = quantized[c]
             tokens = slice(c * CHUNK, (c + 1) * CHUNK)
             ways_out = ((f"res{c}", nc.scalar.copy), (f"acc{c}", nc.vector.tensor_copy if c else nc.scalar.copy))
             for m, (bank, copy_out) in enumerate(ways_out):
                 res = psum.tile([P, CHUNK], F32, name=f"res{c}_{m}", tag=bank)
-                second_product(res[:], m, h_codes, h_bytes)
+                nc.tensor.matmul_mx(
+                    out=res[:],
+                    lhsT=w2_codes[:, 2 * m * P : 2 * (m + 1) * P].bitcast(FP4X4),
+                    lhsT_scale=w2_bytes[:, m * P : (m + 1) * P],
+                    rhs=h_codes[:].bitcast(FP8X4),
+                    rhs_scale=h_bytes[:],
+                    start=True,
+                    stop=True,
+                )
                 copy_out(out=staged[m][:, tokens], in_=res[:])
-                if m and c == CHUNKS - 2:
-                    continue
-                stored = slice((c - 1) * CHUNK, S) if m and c == CHUNKS - 1 else tokens
-                nc.sync.dma_start(out=out_rows[:, m, stored], in_=staged[m][:, stored])
+                joined = m == M_TILES - 1 and c >= CHUNKS - 2
+                if not joined:
+                    nc.sync.dma_start(out=out_rows[:, m, tokens], in_=staged[m][:, tokens])
+        both = slice(S - 2 * CHUNK, S)
+        nc.sync.dma_start(out=out_rows[:, M_TILES - 1, both], in_=staged[M_TILES - 1][:, both])

@@ -213,8 +213,4 @@ def tile_picked_posadd_gelu_p_kernel(tc, x_words, x_scales, w1, w2_words, w2_sca
                     stop=True,
                 )
                 copy_out(out=staged[m][:, tokens], in_=res[:])
-                joined = m == M_TILES - 1 and c >= CHUNKS - 2
-                if not joined:
-                    nc.sync.dma_start(out=out_rows[:, m, tokens], in_=staged[m][:, tokens])
-        both = slice(S - 2 * CHUNK, S)
-        nc.sync.dma_start(out=out_rows[:, M_TILES - 1, both], in_=staged[M_TILES - 1][:, both])
+                nc.sync.dma_start(out=out_rows[:, m, tokens], in_=staged[m][:, tokens])

@@ -94,7 +94,9 @@ def tile_picked_posadd_gelu_p_kernel(tc, x_words, x_scales, w1, w2_words, w2_sca
         w2_codes = shared.tile([P, 2 * N], U8, name="w2_codes", offset=W2_AT, align_bytes=ALIGN)
         w2_bytes = shared.tile([P, N], U8, name="w2_bytes", offset=W2_AT + 2 * N, align_bytes=ALIGN)
         nc.vector.memset(w2_bytes[:].bitcast(I32), 0)
-        nc.sync.dma_start(out=w2_codes[:].bitcast(I32), in_=w2_words[0].bitcast(I32))
+        for m in range(M_TILES):
+            half = slice(2 * m * P, 2 * (m + 1) * P)
+            nc.sync.dma_start(out=w2_codes[:, half].bitcast(I32), in_=w2_words[0, :, half].bitcast(I32))
         for q in range(QUADS):
             nc.sync.dma_start(
                 out=w2_bytes[QUAD * q : QUAD * q + ROWS, :].bitcast(I32),
@@ -194,7 +196,7 @@ def tile_picked_posadd_gelu_p_kernel(tc, x_words, x_scales, w1, w2_words, w2_sca
             nc.scalar.activation(hidden[:, final_from + first : final_from + last, PAIR:], final_pair[:, first:last, :], GELU)
 
         out_rows = out.rearrange("(m p) j -> p m j", p=P)
-        staged = [held.tile([P, S], F32, name=f"staged{m}") for m in range(M_TILES)]
+        staged = held.tile([P, M_TILES, S], F32, name="staged")
         for c in range(CHUNKS):
             if c not in quantized:
                 quantized[c] = quantize_hidden(c, last_cuts if c == CHUNKS - 1 else whole)
@@ -212,5 +214,8 @@ def tile_picked_posadd_gelu_p_kernel(tc, x_words, x_scales, w1, w2_words, w2_sca
                     start=True,
                     stop=True,
                 )
-                copy_out(out=staged[m][:, tokens], in_=res[:])
-                nc.sync.dma_start(out=out_rows[:, m, tokens], in_=staged[m][:, tokens])
+                copy_out(out=staged[:, m, tokens], in_=res[:])
+                if c != 1:
+                    nc.sync.dma_start(out=out_rows[:, m, tokens], in_=staged[:, m, tokens])
+            if c == 1:
+                nc.sync.dma_start(out=out_rows[:, :, tokens], in_=staged[:, :, tokens])

import itertools
from contextlib import ExitStack

import concourse.mybir as mybir

K, T, S, H, N = 1024, 2048, 512, 512, 256
FLOPS = 2 * K * H * S + 2 * H * N * S

F32 = mybir.dt.float32
BF16 = mybir.dt.bfloat16
I32 = mybir.dt.int32
U32 = mybir.dt.uint32
U16 = mybir.dt.uint16
U8 = mybir.dt.uint8
FP8X4 = mybir.dt.float8_e4m3fn_x4
FP4X4 = mybir.dt.float4_e2m1fn_x4
GELU = mybir.ActivationFunctionType.Gelu_apprx_tanh
COPY = mybir.ActivationFunctionType.Copy
ADD = mybir.AluOpType.add

P = 128
PACK = 4
K_PASS = P * PACK
PASSES = K // K_PASS
QUADS = 4
QUAD = P // QUADS
ROWS = 4
LIST_COL = 16
PAIR = 2
LAST = PACK - 1
CHUNK = 128
CHUNKS = S // CHUNK
PIECE = CHUNK // 2
M_TILES = N // P
WARM = 8
ALIGN = 64

SPREAD_FROM, SPREAD = 32, 2

TABLE = 4 * T
GROUPED = 2 * PACK * H
W2_BYTES = 3 * N
GROUPED_AT = PAIR * TABLE
XS_TABLE_AT = GROUPED_AT - T // 2
W2_AT = GROUPED_AT + GROUPED + TABLE
TABLE_AT = {2: GROUPED_AT + GROUPED, 3: W2_AT + W2_BYTES}


def tile_picked_posadd_gelu_p_kernel(tc, x_words, x_scales, w1, w2_words, w2_scales, pe, offs, out):
    nc = tc.nc
    with ExitStack() as ctx:
        held = ctx.enter_context(tc.tile_pool(name="held", bufs=1))
        shared = ctx.enter_context(tc.tile_pool(name="shared", bufs=1))
        psum = ctx.enter_context(tc.psum_pool(name="psum", bufs=1))

        offsets = held.tile([P, S // LIST_COL], U16, name="offsets")
        w1_raw = held.tile([P, PASSES, PACK, H], F32, name="w1_raw")
        x_table = held.tile([P, PASSES, T], I32, name="x_table", align_bytes=ALIGN)
        xs_table = shared.tile([P, T], U8, name="xs_table", offset=XS_TABLE_AT)
        xs_plane = held.tile([P, S], U8, name="xs_plane", align_bytes=ALIGN)

        nc.vector.memset(xs_table[:].bitcast(I32), 0)

        warm = held.tile([P, 2, WARM], F32, name="warm")
        nc.vector.memset(warm[:, 0, :], 0.0)
        nc.scalar.activation(warm[:, 1, :], warm[:, 0, :], GELU)

        nc.sync.dma_start(
            out=w1_raw[:].rearrange("p z j c -> p z (j c)"), in_=w1.rearrange("(z p j) c -> p z (j c)", z=PASSES, j=PACK)
        )
        nc.sync.dma_start(
            out=xs_table[SPREAD_FROM : SPREAD_FROM + SPREAD * PASSES * QUADS * ROWS : SPREAD].bitcast(I32),
            in_=x_scales.rearrange("z r c -> r z c").bitcast(I32),
        )
        nc.sync.dma_start(offsets[:], offs)
        nc.sync.dma_start(out=x_table[:], in_=x_words.rearrange("z p c r -> p z (c r)").bitcast(I32))

        xs_picked = shared.tile([P, W2_BYTES + 2 * ALIGN], U8, name="xs_picked", offset=W2_AT - ALIGN)
        nc.vector.tensor_copy(xs_picked[:, :S], xs_table[:].indirect(offsets[:]))
        for r in range(ROWS):
            first = SPREAD_FROM + SPREAD * PASSES * r
            nc.sync.dma_start(
                out=xs_plane[r:P:ROWS].bitcast(I32),
                in_=xs_picked[first : first + SPREAD * (P // ROWS) : SPREAD, :S].bitcast(I32),
            )

        first_tables = shared.tile([P, PAIR * T], F32, name="pe_table01", offset=0)
        nc.sync.dma_start(out=first_tables[:], in_=pe.rearrange("(p u e) c -> u p (e c)", u=PACK // PAIR, e=PAIR)[0])
        pe_table = {0: first_tables}
        for t in range(PAIR, PACK):
            pe_table[t] = shared.tile([P, T], F32, name=f"pe_table{t}", offset=TABLE_AT[t])
            nc.sync.dma_start(out=pe_table[t][:], in_=pe.rearrange("(p t) c -> t p c", t=PACK)[t])

        w2_codes = shared.tile([P, 2 * N], U8, name="w2_codes", offset=W2_AT, align_bytes=ALIGN)
        w2_bytes = shared.tile([P, N], U8, name="w2_bytes", offset=W2_AT + 2 * N, align_bytes=ALIGN)
        nc.vector.memset(w2_bytes[:].bitcast(I32), 0)
        for m in range(M_TILES):
            half = slice(2 * m * P, 2 * (m + 1) * P)
            nc.sync.dma_start(out=w2_codes[:, half].bitcast(I32), in_=w2_words[0, :, half].bitcast(I32))
        for q in range(QUADS):
            nc.sync.dma_start(
                out=w2_bytes[QUAD * q : QUAD * q + ROWS, :].bitcast(I32),
                in_=w2_scales[0, ROWS * q : ROWS * (q + 1), :].bitcast(I32),
            )

        acc = [psum.tile([P, S], F32, name=f"acc{t}", tag=f"acc{t}") for t in range(PACK)]
        grouped_tiles = (
            lambda: held.tile([P, PACK, P, PACK], BF16, name="w1_grouped0", align_bytes=ALIGN),
            lambda: shared.tile([P, PACK, P, PACK], BF16, name="w1_grouped1", offset=GROUPED_AT, align_bytes=ALIGN),
        )
        operands = []
        for z, round_copy in enumerate((nc.scalar.copy, nc.vector.tensor_copy)):
            grouped = grouped_tiles[z]()
            round_copy(out=grouped[:].rearrange("p t m j -> p m j t"), in_=w1_raw[:, z].rearrange("p j (m t) -> p m j t", t=PACK))
            w1_codes = held.tile([P, H], U32, name=f"w1_codes{z}", align_bytes=ALIGN)
            w1_bytes = held.tile([P, H], U8, name=f"w1_bytes{z}", align_bytes=ALIGN)
            nc.vector.quantize_mx(
                out=w1_codes[:].bitcast(FP8X4), scales=w1_bytes[:], in_=grouped[:].rearrange("p t m j -> p (t m j)")
            )
            x_picked = held.tile([P, S], U32, name=f"x_picked{z}", align_bytes=ALIGN)
            nc.vector.tensor_copy(x_picked[:], x_table[:, z, :].bitcast(U32).indirect(offsets[:]))
            operands.append((w1_codes, w1_bytes, x_picked))

        for groups, z, e in itertools.product(((0, LAST), (2, 1)), range(PASSES), range(PAIR)):
            t = groups[e]
            columns = slice(t * P, (t + 1) * P)
            w1_codes, w1_bytes, x_picked = operands[z]
            nc.tensor.matmul_mx(
                out=acc[t][:],
                lhsT=w1_codes[:, columns].bitcast(FP8X4),
                lhsT_scale=w1_bytes[:, columns],
                rhs=x_picked[:].bitcast(FP8X4),
                rhs_scale=xs_plane[ROWS * z : P, :],
                start=(z == 0),
                stop=(z == PASSES - 1),
            )

        sums = {t: held.tile([P, S], F32, name=f"sums{t}") for t in (0, LAST)}
        nc.scalar.copy(out=sums[0][:], in_=acc[0][:])
        nc.vector.tensor_copy(out=sums[LAST][:], in_=acc[LAST][:])
        pe_picked = held.tile([P, S], F32, name="pe_picked")
        nc.scalar.activation(pe_picked[:], first_tables[:, T:].indirect(offsets[:]), COPY)

        pre = [held.tile([P, PAIR, S], F32, name=f"pre{u}") for u in range(PACK // PAIR)]
        hidden = held.tile([P, S, PACK], BF16, name="hidden", align_bytes=ALIGN)

        def looked_up(t, first, last):
            return pe_table[t][:].indirect(offsets[:, first // LIST_COL : last // LIST_COL])

        def add_pe(t, first, last):
            nc.vector.tensor_tensor(pre[t // PAIR][:, t % PAIR, first:last], looked_up(t, first, last), sums[t][:, first:last], ADD)

        def gelu(u, first, last):
            nc.scalar.activation(
                hidden[:, first:last, PAIR * u : PAIR * (u + 1)], pre[u][:, :, first:last].rearrange("p e j -> p j e"), GELU
            )

        def quantize_hidden(c, cuts):
            h_codes = held.tile([P, CHUNK], U32, name=f"h_codes{c}", align_bytes=ALIGN)
            h_bytes = held.tile([P, CHUNK], U8, name=f"h_bytes{c}", align_bytes=ALIGN)
            for first, last in zip(cuts[:-1], cuts[1:]):
                nc.vector.quantize_mx(
                    out=h_codes[:, first:last].bitcast(FP8X4),
                    scales=h_bytes[:, first:last],
                    in_=hidden[:, c * CHUNK + first : c * CHUNK + last, :].rearrange("p n t -> p (n t)"),
                )
            return h_codes, h_bytes

        add_pe(0, 0, S)
        sums[2] = shared.tile([P, S], F32, name="sums2", offset=0)
        nc.scalar.copy(out=sums[2][:], in_=acc[2][:])
        nc.vector.tensor_tensor(pre[0][:, 1, :], acc[1][:], pe_picked[:], ADD)
        for c in range(CHUNKS):
            gelu(0, c * CHUNK, (c + 1) * CHUNK)
        add_pe(2, 0, S)

        final_from = S - PIECE
        fetched_from = final_from - 2 * PIECE
        fetched = held.tile([P, final_from - fetched_from], F32, name="fetched")
        nc.scalar.activation(fetched[:], looked_up(LAST, fetched_from, final_from), COPY)
        for first in range(0, fetched_from, PIECE):
            add_pe(LAST, first, first + PIECE)
            gelu(1, first, first + PIECE)
        nc.vector.tensor_tensor(pre[1][:, 1, fetched_from:final_from], fetched[:], sums[LAST][:, fetched_from:final_from], ADD)
        for first in range(fetched_from, final_from, PIECE):
            gelu(1, first, first + PIECE)

        whole = (0, CHUNK)
        quantized = {0: quantize_hidden(0, whole)}
        nc.vector.tensor_tensor(pre[1][:, 1, PIECE:CHUNK], looked_up(LAST, final_from, S), sums[LAST][:, final_from:], ADD)
        apart = S + PIECE - final_from
        final_pair = pre[1][:].rearrange("p e j -> p (e j)")[:, final_from : final_from + PAIR * apart].rearrange("p (e j) -> p j e", e=PAIR)
        last_cuts = (0, PIECE, PIECE + PIECE // 2, CHUNK)
        for first in range(0, PIECE, PIECE // 2):
            last = first + PIECE // 2
            nc.scalar.activation(hidden[:, final_from + first : final_from + last, PAIR:], final_pair[:, first:last, :], GELU)

        out_rows = out.rearrange("(m p) j -> p m j", p=P)
        staged = held.tile([P, M_TILES, S], F32, name="staged")
        for c in range(CHUNKS):
            if c not in quantized:
                quantized[c] = quantize_hidden(c, last_cuts if c == CHUNKS - 1 else whole)
            h_codes, h_bytes = quantized[c]
            tokens = slice(c * CHUNK, (c + 1) * CHUNK)
            ways_out = ((f"res{c}", nc.scalar.copy), (f"acc{c}", nc.vector.tensor_copy if c else nc.scalar.copy))
            for m, (bank, copy_out) in enumerate(ways_out):
                res = psum.tile([P, CHUNK], F32, name=f"res{c}_{m}", tag=bank)
                nc.tensor.matmul_mx(
                    out=res[:],
                    lhsT=w2_codes[:, 2 * m * P : 2 * (m + 1) * P].bitcast(FP4X4),
                    lhsT_scale=w2_bytes[:, m * P : (m + 1) * P],
                    rhs=h_codes[:].bitcast(FP8X4),
                    rhs_scale=h_bytes[:],
                    start=True,
                    stop=True,
                )
                copy_out(out=staged[:, m, tokens], in_=res[:])
                if c != 1:
                    nc.sync.dma_start(out=out_rows[:, m, tokens], in_=staged[:, m, tokens])
            if c == 1:
                nc.sync.dma_start(out=out_rows[:, :, tokens], in_=staged[:, :, tokens])
